import numpy as np, ml_dtypes
CORES = [2,6,10,14,18,22,26,30]
N = 8
import mx_ref
BF = ml_dtypes.bfloat16
def pick(q, e):
    c = np.concatenate([q[0].reshape(128, -1, 4), np.zeros((128, 1, 4), np.uint8)], axis=1); s = np.concatenate([q[1], np.ones((16, 1), np.uint8)], axis=1)
    return (np.ascontiguousarray(c[:, e].reshape(128, -1)), np.ascontiguousarray(s[:, e]))
def join(*qs):
    return (np.concatenate([q[0] for q in qs], axis=1), np.concatenate([q[1] for q in qs], axis=1))
def put(q, e, v):
    c, s = q[0].reshape(128, -1, 4).copy(), q[1].copy(); c[:, e] = v[0].reshape(128, -1, 4); s[:, e] = v[1]
    return (c.reshape(128, -1), s)
def pk(c, s):
    return (np.ascontiguousarray(c), mx_ref.live(s))
def emit(q):
    return q[0], q[1]
def cols(t, e):
    v = np.concatenate([t.reshape(128, -1, 4), np.zeros((128, 1, 4), BF)], axis=1)
    return np.ascontiguousarray(v[:, e]).reshape(128, -1)
def tile(rs):
    return np.stack(rs, axis=2).reshape(128, -1).astype(BF)
def cut(t, i, w=512):
    return t[:, w * i:w * i + w]
def f(rng, *shape):
    return mx_ref.flush((rng.standard_normal(shape, dtype=np.float32) * np.exp2(rng.integers(-2, 3, shape[:-1] + (1,)))).astype(BF))
def wide(rng, *shape, cols=0):
    v = rng.standard_normal(shape, dtype=np.float32) * np.exp2(rng.integers(-12, 13, shape)).astype(np.float32)
    if cols: v *= np.repeat(np.exp2(rng.integers(-cols, cols + 1, shape[:-2] + (1, shape[-1] // 4))) * (rng.random(shape[:-2] + (1, shape[-1] // 4)) > 0.0625), 4, axis=-1).astype(np.float32)
    return mx_ref.flush(v.astype(BF))
P, K, O = 192, 64, 1
E = P + 2 * K // N
def play(x, u, a, b):
    row = mx_ref.quantize(np.concatenate([x[r] for r in range(N)], axis=1))
    num = 4 * np.arange(N * P)
    k = mx_ref.quantize(np.ascontiguousarray(u[0]))
    high = []
    for t in range(2):
        n = num.size
        s = mx_ref.matmul(k, row)[0] + np.float32(0)
        split = np.sort(np.argsort(-s, kind="stable")[:K])
        parents = pick(row, split)
        kids = []
        for m in (a[0], b[0]):
            kids.append(tile([mx_ref.matmul(mx_ref.quantize(np.ascontiguousarray(cut(m, i))), parents) * np.float32(0.0625) for i in range(4)]))
        size = np.max(np.abs(np.stack(kids).astype(np.float32)).reshape(2, 16, 8, K, 4), axis=(2, 4))
        high.append((np.max(np.abs(s)), np.max(size), np.min(np.where(size == 0, np.float32(1), size))))
        e = np.repeat(np.arange(n), 1 + np.isin(np.arange(n), split))
        first = split + np.arange(K)
        num = num[e]
        num[first + 1] += 2 - t
        e[first] = n + np.arange(K)
        e[first + 1] = n + K + np.arange(K)
        row = pick(join(row, mx_ref.quantize(kids[0]), mx_ref.quantize(kids[1])), e)
    return row, num, high
def times(t, v):
    return mx_ref.flush((t.astype(np.float32) * np.float32(v)).astype(BF))
def lift(d, r, e, v):
    s = np.where(d["u"][0][:, None, :4].astype(np.float32) < 0, -v, v)
    x = np.array(d["x"][r].astype(np.float32)).reshape(128, P, 4)
    x[:, e] = np.abs(x[:, e]) * s
    d["x"][r] = mx_ref.flush(x.reshape(128, -1).astype(BF))
def setup_inputs(rng):
    u = np.array(f(rng, 128, 512))
    u[:, 4:] = 0
    return {"x": np.array(f(rng, N, 128, 4 * P)), "u": np.stack([u] * N), "a": np.stack([f(rng, 128, 2048)] * N), "b": np.stack([f(rng, 128, 2048)] * N), "w": f(rng, N, 128, 512 * O)}
def setup_inputs_below(rng):
    d = setup_inputs(rng)
    d["x"] = np.array(times(d["x"], 2.0 ** 20))
    for r in range(N): lift(d, r, np.arange(P), -1)
    lift(d, N - 1, rng.permutation(P)[:K], -2.0 ** -6)
    v, p = d["a"][0].astype(np.float32) * np.float32(2.0 ** -6), np.arange(128)
    for i in range(4): v[p, 512 * i + 4 * p + i] = 128
    d["a"] = np.stack([mx_ref.flush(v.astype(BF))] * N)
    d["b"] = times(d["a"], 2.0 ** -4)
    return d
def setup_inputs_edge(rng):
    d = setup_inputs(rng)
    d["a"], d["b"], d["x"] = times(d["a"], 2.0 ** -12), times(d["b"], 2.0 ** -12), np.array(times(d["x"], 64))
    lift(d, int(rng.integers(1, N - 1)), rng.permutation(P)[:K], 4096)
    lift(d, N - 1, rng.permutation(P)[:K], 64)
    return d
def setup_inputs_spread(rng):
    return {**setup_inputs(rng), "x": wide(rng, N, 128, 4 * P, cols=6)}
def setup_inputs_ties(rng):
    d = setup_inputs(rng)
    v, e = times(f(rng, 128, 24), 2.0 ** 14), (rng.permutation(N * P) % 6).reshape(N, P)
    d["x"] = np.stack([cols(v, e[r]) for r in range(N)])
    lift(d, N - 1, rng.permutation(P)[:K // 8], 64)
    return {**d, "b": d["a"].copy()}
def setup_inputs_zero(rng):
    d = setup_inputs(rng)
    d["u"][:, 64:] = 0
    for r in range(N):
        kind = rng.permutation(P) % 3
        lift(d, r, np.flatnonzero(kind == 2), -1)
        x = np.array(d["x"][r]).reshape(128, P, 4)
        x[:, kind == 0] = 0
        x[:64, kind == 1] = 0
        d["x"][r] = x.reshape(128, -1)
    return d
def check_inputs(d):
    b = []
    for k in ("x", "u", "a", "b", "w"):
        v = np.abs(d[k].astype(np.float32))
        if not (np.isfinite(v).all() and ((v == 0) | (v >= 2.0 ** -30) & (v <= 2.0 ** 30)).all()): b.append("a value of " + k)
    if (d["u"][:, :, 4:].astype(np.float32) != 0).any(): b.append("u has numbers behind its column 0")
    for k in ("u", "a", "b"):
        v = d[k].astype(np.float32)
        if (v != v[:1]).any(): b.append(k + " differs between ranks")
    if not b:
        try:
            high = play(d["x"], d["u"], d["a"], d["b"])[2]
            if not all(np.isfinite(s) for s, c, m in high): b.append("a score")
            if not all(c <= 2.0 ** 30 and m >= 2.0 ** -30 for s, c, m in high): b.append("a number of a child")
        except Exception:
            b.append("a number of a child")
    return b
def reference(x, u, a, b, w):
    row, num, _ = play(x, u, a, b)
    oc, osc = np.zeros((N, 128, 4 * E), np.uint8), np.zeros((N, 16, E), np.uint8)
    hs, y = np.zeros((N, 1, E), np.float32), np.zeros((N, 128, O * E), np.float32)
    for r in range(N):
        q = pick(row, np.arange(r * E, r * E + E))
        oc[r], osc[r] = emit(q)
        hs[r, 0] = num[r * E:r * E + E]
        for o in range(O):
            y[r, :, o * E:o * E + E] = mx_ref.matmul(mx_ref.quantize(np.ascontiguousarray(cut(w[r], o))), q)
    return {"oc": oc, "osc": osc, "hs": hs, "y": y}

@@ -1,0 +1,617 @@
+from concourse.bass import DstId, RemoteDMATransfer
+from concourse.mybir import dt, AluOpType, AxisListType, ActivationFunctionType
+
+ALU = AluOpType
+ACT = ActivationFunctionType
+N, P, K, E = 8, 192, 64, 208
+WMAX = 336
+TAU = 2.0 ** -106
+BIG = 65536.0
+DUMP = 1720
+ROW = 8 + 4 * DUMP
+CW = 416
+HW = CW // 2
+NV = 4
+
+SMALL = {}
+for _n, _w in dict(PB=6, PZ=6, LO=2, HI=2, QOB=1, NST=2, RK=6, KEYC=6, KEYN=6, V2C=6, VV=4, FL=1, F2=1, TH=1, KB=1, NB=1, TK=1,
+                   PID=1, BITS=4, SG=1, ISC=1, CK=1, I2=1, NT=1, NTB=1, NTN=6, S1A=1, C2A=1, KES=1, KE=3, DB=3, DBN=1, NKA=1, NKE=1,
+                   CN=1, BN=1, EB=1, S1=1, C2=1, A12=1, SB1=1, SGN=1, AN=1, INI=1, CLA=1, CLP=1, CLM=1, CLB=1, BL1=1, BL2=1, GRP=1,
+                   GR=1, ZS=8, HS=8, JJ=16, JK=8).items():
+    SMALL[_n] = (8 * sum((w + 7) // 8 for _, w in SMALL.values()), _w)
+
+
+def _scratch():
+    f, h, q, s = "float32", "bfloat16", "float8_e4m3fn_x4", "uint8"
+    d = {}
+
+    def sb(dtype, **kw):
+        for name, n in kw.items():
+            d[name] = ("sbuf", [128, n], dtype)
+    sb(h, XB=4 * P, U4=4, UB=512, AB=2048, BB=2048, WB=512, KH1=4 * P, KH2=4 * P, FH1=576, FH2=576,
+       GH1=512, GH2=512, CM=6 * CW, SCN=6 * HW, J1=2 * CW, M1=192, M2=160, Z0=128)
+    for name, n in dict(UQ=128, AQ=512, BQ=512, WQ=128, W1=3 * WMAX, HQ=144, HK1=144, HK2=144, PK=128, W2=4 * WMAX + 256, FQ=E).items():
+        d[name] = ("sbuf", [128, n], q)
+        d[name + "S"] = ("sbuf", [128, n], s)
+    sb(f, BLT=32, C64=32, THT=32, OC=8, OCB=64, TOWN=64, ST0=192, DL=384, TI0=64, TIE=384, land1=24, LB=352, LT=352,
+       SLT=32, SLT2=32, VALT=192, AD=192, EV=576, ET=576, land2=412, RBS=64, RBK=64, SC=192, KY=192, E1=192, E2=160, NK1=192,
+       NK2=160, R1=96, R2=80, FB=64, FR=256, Q1=256, Q2=256, VA=64, VB=64, CTI=32, CT=32, SEC=32, RA=ROW, RB=ROW, XS=256, XT=256,
+       ZT=32, XR=32, YY=64, YT=64, HT=4 * WMAX + 256, HR=E, GD=128, GE=128, GT=128, YS=E, J3=416, OI2=22,
+       SM=8 * sum((w + 7) // 8 for _, w in SMALL.values()))
+    sb("int32", OI=26, PIN=1, PA=4)
+    sb("uint16", OU=26, OD=20, OV=2, OFF=4, OFFG=8, OFFL=14)
+    d["PS"] = ("psum", [128, 4096], f)
+    return d
+
+
+SCRATCH = _scratch()
+SEMAPHORES = ["cv", "cs", "ct", "cg", "loc", "ar1", "ar2", "arh"] + ["d%d" % i for i in range(40)]
+
+
+def _halo(r):
+    return (0 if r == 0 else 128 - 16 * r), (0 if r == N - 1 else 16 + 16 * r)
+
+
+def _land(r):
+    hL, hR = _halo(r)
+    return ("HQ", 0, hL) if hL and hR else ("W1", 0, hL + P)
+
+
+def rank_program(g, core, T, topo):
+    r = T.rank_of(core)
+    if r is None:
+        return
+    hL, hR = _halo(r)
+    Wn = hL + P + hR
+    ws = P * r - hL
+    G1, G2, G3 = 3 * Wn, 3 * Wn + 128, 3 * Wn + 256
+    e0 = E * r + 8
+    q_of = {"v": g.vector, "s": g.scalar, "t": g.tensor, "g": g, "y": g.sync}
+    cnt = {"cv": 0, "cs": 0, "ct": 0, "cg": 0}
+    known = {k: {} for k in q_of}
+    recs = {}
+    total = {}
+    ndma, loc = [0], [0]
+
+    def C(name, c0=0, c1=None, p0=0, p1=128, step=1):
+        if name in SMALL:
+            o, w = SMALL[name]
+            c0, c1, name = o + c0, o + (w if c1 is None else c1), "SM"
+        elif c1 is None:
+            c1 = SCRATCH[name][1][-1]
+        ap = T[name][p0:p1, c0:c1] if step == 1 else T[name][p0:p1, c0:c1:step]
+        return (ap, name, p0, p1, c0, c1)
+
+    def H(name, c0=0, c1=None):
+        return C(name, c0, c1, 0, 64)
+
+    def U(name, c0=0, c1=None):
+        return C(name, c0, c1, 64, 128)
+
+    def Q(name, q, c0=0, c1=None):
+        return C(name, c0, c1, 32 * q, 32 * q + 32)
+
+    def part_of(name, i, n, step):
+        w = n // step
+        return (T[name][:, i:n:step], name, 0, 128, i * w, i * w + w)
+
+    def bank(k, n, p0=0, p1=128, c0=0):
+        return (T.PS[p0:p1, 512 * k + c0:512 * k + n], "PS", 0, 128, 512 * k, 512 * k + 512)
+
+    def ext(ap):
+        return (ap, None, 0, 0, 0, 0)
+
+    def need(q, sem, val, snap):
+        if known[q].get(sem, 0) >= val:
+            return
+        q_of[q].wait_ge(T.sem[sem], val)
+        for k, x in list(snap.items()) + [(sem, val)]:
+            known[q][k] = max(known[q].get(k, 0), x)
+
+    def deps(q, reads, writes):
+        todo = {}
+        for view, wr in [(x, False) for x in reads] + [(x, True) for x in writes]:
+            _, name, p0, p1, c0, c1 = view
+            for (a0, a1, b0, b1, kind, rq, sem, val, snap) in recs.get(name, []):
+                if a0 >= p1 or p0 >= a1 or b0 >= c1 or c0 >= b1:
+                    continue
+                if not kind and (rq == q or (not wr and name != "PS")):
+                    continue
+                if val > todo.get(sem, (0, 0))[0]:
+                    todo[sem] = (val, snap)
+        for sem in sorted(todo, key=lambda k: -len(todo[k][1])):
+            need(q, sem, todo[sem][0], todo[sem][1])
+
+    def note(q, rq, sem, val, reads, writes):
+        snap = dict(known[q])
+        snap[sem] = val
+        for view, wr in [(x, False) for x in reads] + [(x, True) for x in writes]:
+            _, name, p0, p1, c0, c1 = view
+            lst = recs.setdefault(name, [])
+            if wr:
+                lst[:] = [x for x in lst if not (x[0] >= p0 and x[1] <= p1 and x[2] >= c0 and x[3] <= c1)]
+            lst.append((p0, p1, c0, c1, wr, rq, sem, val, snap))
+        total[sem] = val
+
+    def run(q, f, reads, writes):
+        deps(q, reads, writes)
+        sem = "c" + q
+        cnt[sem] += 1
+        f().then_inc(T.sem[sem], 1)
+        note(q, q, sem, cnt[sem], reads, writes)
+
+    def dma(q, out, in_, bits=0):
+        w, x = [out] if out[1] else [], [in_] if in_[1] else []
+        deps(q, x, w)
+        sem = "d%d" % ndma[0]
+        ndma[0] += 1
+        o = out[0].bitcast(dt.uint8) if bits & 1 else out[0]
+        i = in_[0].bitcast(dt.uint8) if bits & 2 else in_[0]
+        q_of[q].dma_start(o, i).then_inc(T.sem[sem], 16)
+        note(q, "dma", sem, 16, x, w)
+
+    def move(dst, d0, src, s0, n):
+        if n:
+            dma("y", C(dst, d0, d0 + n), C(src, s0, s0 + n), bits=3)
+            dma("y", C(dst + "S", d0, d0 + n), C(src + "S", s0, s0 + n))
+
+    def memset(o, val):
+        run("v", lambda: g.vector.memset(o[0], val), [], [o])
+
+    def copy(q, o, i):
+        run(q, (lambda: g.vector.tensor_copy(o[0], i[0])) if q == "v" else (lambda: g.scalar.activation(o[0], i[0], ACT.Copy)), [i], [o])
+
+    def scaled(q, o, i, f):
+        run(q, (lambda: g.vector.tensor_scalar(o[0], i[0], f, None, ALU.mult)) if q == "v" else
+            (lambda: g.scalar.activation(o[0], i[0], ACT.Copy, scale=f)), [i], [o])
+
+    def ts(o, i, s1, op0, s2=None, op1=None):
+        rd = [i] + [x for x in (s1, s2) if isinstance(x, tuple)]
+        a = s1[0] if isinstance(s1, tuple) else s1
+        b = s2[0] if isinstance(s2, tuple) else s2
+        run("v", (lambda: g.vector.tensor_scalar(o[0], i[0], a, None, op0)) if op1 is None else
+            (lambda: g.vector.tensor_scalar(o[0], i[0], a, b, op0, op1)), rd, [o])
+
+    def tt(o, a, b, op):
+        run("v", lambda: g.vector.tensor_tensor(o[0], a[0], b[0], op), [a, b], [o])
+
+    def tr(o, i):
+        run("v", lambda: g.vector.transpose(o[0], i[0]), [i], [o])
+
+    def total_of(q, o, i, junk=None):
+        if q == "v":
+            run("v", lambda: g.vector.tensor_reduce(o[0], i[0], AxisListType.X, ALU.add), [i], [o])
+        else:
+            run("s", lambda: g.scalar.activation(junk[0], i[0], ACT.Copy, accum_out=o[0]), [i], [o, junk])
+
+    def pairsum(o, a, b, start=0.0):
+        run("v", lambda: g.vector.tensor_tensor_scan(o[0], a[0], b[0], start, ALU.add, ALU.add), [a, b], [o])
+
+    def affine(o, i, bias, scale, func=ACT.Identity, acc=None):
+        rd = [i] + [x for x in (bias, scale) if isinstance(x, tuple)]
+        b = bias[0] if isinstance(bias, tuple) else bias
+        a = scale[0] if isinstance(scale, tuple) else scale
+        if acc is None:
+            run("s", lambda: g.scalar.activation(o[0], i[0], func, bias=b, scale=a), rd, [o])
+        else:
+            run("s", lambda: g.scalar.activation(o[0], i[0], func, bias=b, scale=a, accum_out=acc[0]), rd, [o, acc])
+
+    def gather(q, o, win, off):
+        src = win[0].indirect(off[0])
+        run(q, (lambda: g.vector.tensor_copy(o[0], src)) if q == "v" else (lambda: g.scalar.activation(o[0], src, ACT.Copy)), [win, off], [o])
+
+    def gathered(o, win, off, bias, scale, func):
+        src = win[0].indirect(off[0])
+        run("s", lambda: g.scalar.activation(o[0], src, func, bias=bias, scale=scale), [win, off], [o])
+
+    def scatter(win, off, i):
+        run("v", lambda: g.vector.tensor_copy(win[0].indirect(off[0]), i[0]), [i, off], [win])
+
+    def quant(name, c0, c1, src):
+        o, s = C(name, c0, c1), C(name + "S", c0, c1)
+        run("v", lambda: g.vector.quantize_mx(o[0], s[0], src[0]), [src], [o, s])
+
+    def mm(o, l, lc, x, x0, x1):
+        a, b, c, d = C(l, lc, lc + 128), C(l + "S", lc, lc + 128), C(x, x0, x1), C(x + "S", x0, x1)
+        run("t", lambda: g.tensor.matmul_mx(o[0], a[0], b[0], c[0], d[0], True, True), [a, b, c, d], [o])
+
+    part = [False]
+
+    def iota(o, pattern, base, cm, whole=False):
+        now = o[3] - o[2] < 128
+        if now or part[0]:
+            need("g", "cg", cnt["cg"], {})
+        part[0] = now
+        run("g", (lambda: g.iota(o[0], pattern, base, cm)) if whole else
+            (lambda: g.iota(o[0], pattern, base, cm, allow_small_or_imprecise_dtypes=True)), [], [o])
+
+    def pick_codes(o, c0, c1, src, n, off):
+        a, w = C(o, c0, c1), C(src, 0, n)
+        run("v", lambda: g.vector.tensor_copy(a[0].bitcast(dt.uint32), w[0].bitcast(dt.uint32).indirect(off[0])), [w, off], [a])
+
+    def pick_scales(o, c0, c1, src, n, off):
+        gather("s", C(o + "S", c0, c1), C(src + "S", 0, n), off)
+
+    def quadsum(o, h, lo, up, n, between=None):
+        tt(H(h, 0, n), lo, up, ALU.add)
+        if between:
+            between()
+        for q in range(4):
+            tt(Q(o, q, 0, n), Q(h, 0, 0, n), Q(h, 1, 0, n), ALU.add)
+
+    def swap(name):
+        copy("s", H(name, 64, 96), U(name, 32, 64))
+        copy("v", U(name, 64, 96), H(name, 32, 64))
+
+    def pairs(name, order):
+        for q in range(4):
+            copy(order[q], Q(name, q, 96, 192), Q(name, q ^ 1, 0, 96))
+
+    def kids(src, c0, n, t1, t2, first, pat, late=None):
+        for i in range(8):
+            k = (first + i) % 8
+            mm(bank(k, n), "AQ" if i < 4 else "BQ", 128 * (i % 4), src, c0, c0 + n)
+            if i == 7 and late:
+                late()
+            scaled(pat[i], part_of(t1 if i < 4 else t2, i % 4, 4 * n, 4), bank(k, n), 0.0625)
+
+    def ways(a):
+        return topo.engines(a, [c for c in T.cores if topo.chip(c) != topo.chip(a)][0])
+
+    def split(a, b):
+        if topo.chip(a) != topo.chip(b):
+            return topo.engines(a, b)
+        return [e for e in topo.engines(a, b) if e not in ways(a)][:2]
+
+    def arrivals():
+        return sum(len(split(c, core)) for c in T.cores if c != core)
+
+    def fan(src, dst, base, width, arr):
+        deps("g", [src], [])
+        others = [c for c in T.cores if c != core]
+        far = [c for c in others if topo.chip(c) != topo.chip(core)]
+        near = [c for c in others if topo.chip(c) == topo.chip(core)]
+        fe, ne = split(core, far[0]), split(core, near[0])
+
+        def tf(dsts, eng):
+            ids, aps = [], []
+            for c in dsts:
+                d = T.rank_of(c)
+                k = base + width * (r if r < d else r - 1)
+                rid, pid, _ = topo.addr(c)
+                ids.append(DstId(rid=rid, pnc=pid))
+                aps.append(T[dst][:, k:k + width])
+            return RemoteDMATransfer(dst_ids=ids, dma_engine_mask=sum(1 << e for e in eng), remote_sem=T.sem[arr], srcs=[src[0]], dsts=aps)
+        g.remote_dma_fused([tf(far, fe), tf(near, ne)], local_sem=T.sem.loc)
+        loc[0] += len(fe) + len(ne)
+
+    def halo(d, sfx):
+        c = T.cores[d]
+        dst, a, b = _land(d)
+        c0, c1, at = (P - _halo(d)[0], P, a) if d > r else (0, _halo(d)[1], b)
+        rid, pid, _ = topo.addr(c)
+        s = C("W1" + sfx, hL + c0, hL + c1)
+        deps("g", [s], [])
+        o, i = T[dst + sfx][:, at:at + c1 - c0], s[0]
+        if not sfx:
+            o, i = o.bitcast(dt.uint8), i.bitcast(dt.uint8)
+        g.remote_dma(o, i, T.sem.arh, T.sem.loc, pid, rid, sum(1 << e for e in ways(core)))
+        loc[0] += len(ways(core))
+
+    def arrive(sem, val, writes):
+        for _, name, p0, p1, c0, c1 in writes:
+            recs.setdefault(name, []).append((p0, p1, c0, c1, True, "far", sem, val, {sem: val}))
+        total[sem] = val
+
+    dma("s", C("U4"), ext(T.u[:, 0:4]))
+    for name, t in (("XB", T.x), ("AB", T.a), ("BB", T.b), ("WB", T.w)):
+        dma("y", C(name), ext(t[:, :]))
+
+    iota(C("PIN"), [[0, 1]], 0, 1, True)
+    iota(C("RK"), [[64, 6]], 2 * P * r, 0)
+    iota(C("TI0"), [[64, 2], [1, 32]], 0, 0)
+    iota(C("OI", 0, 2), [[0, 2]], 0, 0, True)
+    iota(C("OI", 2, 4), [[0, 2]], 4, 0, True)
+    upper = [(2, 4, -3)]
+    at, nb, na = 4, r, N - 1 - r
+    for what, s0, n in (("main", 0, nb), ("rest", 0, nb), ("rest", nb, na), ("main", nb, na)):
+        if what == "main" and n:
+            iota(C("OI", at, at + 2 * n), [[2, n], [0, 2]], 2 * s0, 0, True)
+            at += 2 * n
+        elif n:
+            m = (n + 1) // 2
+            iota(C("OI", at, at + 2 * m), [[4, m], [0, 2]], 2 * s0 + 1, 0, True)
+            if n // 2:
+                upper.append((at, at + 2 * (n // 2), 2))
+            if n % 2:
+                upper.append((at + n - 1, at + n + 1, 16 - (2 * s0 + 1 + 4 * (m - 1))))
+            at += 2 * m
+    cut = 32 * (nb + (nb + 1) // 2)
+    memset(C("Z0"), 0.0)
+    memset(C("OC"), -9e29)
+    memset(C("land1", 16, 20), -9e29)
+    memset(C("C64"), 64.0)
+    copy("v", C("PID"), C("PIN"))
+    for k, m in enumerate((31, 15, 32, 112)):
+        ts(C("PA", k, k + 1), C("PIN"), m, ALU.bitwise_and)
+    copy("v", C("BITS"), C("PA"))
+    IC, PM16, QO, GR = [C("BITS", k, k + 1) for k in range(4)]
+    affine(C("SG"), C("PID"), -63.5, 1.0, ACT.Sign)
+    affine(C("I2"), IC, 0.0, 2.0)
+    affine(C("TH"), IC, 64.0, -1.0)
+    affine(C("GR"), GR, 0.0, 1.0, ACT.Sign)
+    affine(C("QOB"), QO, float(-4 * HW), 1.0)
+    affine(C("ISC"), C("SG"), 0.0, 1.0, ACT.Relu)
+    affine(C("NT"), C("PID"), C("I2"), -1.0)
+    affine(C("CLA"), PM16, C("PID"), -1.0)
+    affine(C("GRP"), C("GR"), 2.0, -2.0)
+    affine(C("SLT"), C("TI0", 0, 32), C("QOB"), 1.0)
+    affine(C("CK"), C("I2"), C("ISC"), 1.0)
+    affine(C("NTB"), C("NT"), P * r * TAU, -TAU)
+    affine(C("THT"), C("TI0", 0, 32), C("TH"), 0.0)
+    affine(C("SLT2"), C("SLT"), 64.0, 1.0)
+    affine(C("NTN"), C("RK"), C("NTB"), -0.5 * TAU)
+    affine(C("KEYC"), C("RK"), C("CK"), 1.0)
+    affine(U("V2C"), U("RK"), U("I2"), 1.0)
+    affine(C("CLP"), C("CLA"), C("GRP"), 2.0)
+    affine(C("KEYN"), C("KEYC"), 0.0, -1.0)
+
+    for t in range(4):
+        ts(part_of("UB", t, 512, 4), C("Z0"), C("U4", t, t + 1), ALU.add)
+    quant("UQ", 0, 128, C("UB"))
+    quant("W1", hL, hL + P, C("XB"))
+    pieces = [(d, sfx) for sfx in ("S", "") for d in (r - 1, r + 1) if 0 <= d < N]
+    halo(*pieces[0])
+    mm(bank(1, 128), "W1", hL, "UQ", 0, 128)
+    mm(bank(2, 128), "W1", hL + 64, "UQ", 0, 128)
+    mm(bank(0, P), "UQ", 0, "W1", hL, hL + P)
+    copy("v", C("OC", 0, 1), bank(1, 1))
+    copy("v", U("OC", 1, 2), bank(2, 1, 64, 128))
+    copy("v", H("OC", 1, 2), bank(2, 1, 64, 128))
+    fan(C("OC", 0, 2), "land1", 0, 2, "ar1")
+    arrive("ar1", arrivals(), [C("land1", 0, 14)])
+    for piece in pieces[1:]:
+        halo(*piece)
+    want = sum(2 * len(ways(T.cores[d])) for d in (r - 1, r + 1) if 0 <= d < N)
+    hq, hl, hr = _land(r)
+    arrive("arh", want, [C(hq + x, a, b) for x in ("", "S") for a, b in ((hl, hl + hL), (hr, hr + hR)) if b > a])
+    iota(C("OI2", 0, 4), [[16, 2], [0, 2]], 0, 0)
+    iota(C("OI2", 20, 22), [[0, 2]], 32, 0)
+    iota(C("CTI"), [[2 * (G2 - G1) - 2, 2], [2, 16]], 2 * (G1 + ws), 0)
+    for q in range(4):
+        st, sh = (96 if q % 2 == 0 else -96), (32 if q < 2 else -32)
+        iota(Q("OI2", q, 4, 12), [[st, 2], [16, 2], [0, 2]], 96 * (q % 2) + 32 + 32 * (q // 2), 0)
+        iota(Q("OI2", q, 12, 20), [[sh, 2], [st, 2], [16, 2]], 96 * (q % 2) + 32 + 32 * (q // 2), 0)
+
+    copy("v", C("OU"), C("OI"))
+    for c0, c1, x in upper:
+        ts(U("OU", c0, c1), U("OI", c0, c1), float(x), ALU.add)
+    gather("s", C("OCB"), C("OC"), C("OU", 0, 4))
+    tr(C("ST0"), bank(0, P))
+    for k in range(6):
+        affine(C("TIE", 64 * k, 64 * k + 64), C("TI0"), C("NTN", k, k + 1), TAU)
+    tr(C("TOWN"), C("OCB"))
+    quant("AQ", 0, 512, C("AB"))
+    for k in range(6):
+        ts(C("DL", 64 * k, 64 * k + 64), C("TOWN"), C("ST0", 32 * k, 32 * k + 1), ALU.subtract)
+    for k in range(6):
+        tt(C("CM", CW * k + 352, CW * k + CW), C("DL", 64 * k, 64 * k + 64), C("TIE", 64 * k, 64 * k + 64), ALU.is_gt)
+    quant("BQ", 0, 512, C("BB"))
+    copy("s", H("V2C"), C("ST0", 0, 192, 0, 64, 32))
+    affine(C("CLB"), C("ISC"), C("CLP"), 1.0)
+    affine(C("CLM"), C("ISC"), C("CLP"), -1.0)
+    affine(C("CN"), C("ISC"), float(272 + 6 * DUMP), 2.0)
+    affine(C("BL1"), C("ISC"), C("GRP"), -2.0)
+    affine(C("BL2"), C("GRP"), -2.0, 1.0)
+    for k in range(NV, 6):
+        scaled("s", C("NST", k - NV, k - NV + 1), C("ST0", 32 * k, 32 * k + 1), -1.0)
+    affine(C("BLT", 0, 16), C("TI0", 0, 16), C("BL1"), 0.0)
+    affine(C("BLT", 16, 32), C("TI0", 0, 16), C("BL2"), 0.0)
+
+    def last(k):
+        return C("SCN", HW * k + HW - 1, HW * k + HW)
+
+    def tally(k):
+        pairsum(C("SCN", HW * k, HW * k + HW), C("CM", CW * k, CW * k + HW), C("CM", CW * k + HW, CW * k + CW), float(-HW))
+
+    def against(k):
+        sc = C("ST0", 32 * k, 32 * k + 1)
+        if cut > 0:
+            ts(C("CM", CW * k, CW * k + cut), C("LT", 0, cut), sc, ALU.is_ge)
+        if cut < 352:
+            ts(C("CM", CW * k + cut, CW * k + 352), C("LT", cut, 352), sc, ALU.is_gt)
+
+    def signs(k):
+        c, i, j = CW * k, k - NV, CW * (k - NV)
+        affine(C("CM", c, c + 352), C("LT"), C("NST", i, i + 1), 1.0, ACT.Sign)
+        if cut > 0:
+            affine(C("J1", j, j + cut), C("CM", c, c + cut), 0.0, -1.0, ACT.Relu, C("LO", i, i + 1))
+        affine(C("J1", j + cut, j + CW), C("CM", c + cut, c + CW), 0.0, 1.0, ACT.Relu, C("HI", i, i + 1))
+
+    kids("W1", hL, P, "KH1", "KH2", 3, "ssssssss", lambda: gather("s", C("LB", 192, 352), C("land1", 0, 20), C("OU", 16, 26)))
+    quant("W1", Wn + hL, Wn + hL + P, C("KH1"))
+    gather("v", C("LB", 0, 192), C("land1", 0, 20), C("OU", 4, 16))
+    tr(C("LT", 0, 192), C("LB", 0, 192))
+    tr(C("LT", 192, 352), C("LB", 192, 352))
+    mm(bank(3, P), "UQ", 0, "W1", Wn + hL, Wn + hL + P)
+    signs(4)
+    signs(5)
+    against(0)
+    against(1)
+    tally(0)
+    quant("W1", 2 * Wn + hL, 2 * Wn + hL + P, C("KH2"))
+    mm(bank(4, P), "UQ", 0, "W1", 2 * Wn + hL, 2 * Wn + hL + P)
+    against(2)
+    tally(1)
+    against(3)
+    tally(2)
+    tally(3)
+    for k in range(NV, 6):
+        i = k - NV
+        if cut > 0:
+            ts(last(k), C("HI", i, i + 1), C("LO", i, i + 1), ALU.subtract, float(cut - HW), ALU.add)
+        else:
+            ts(last(k), C("HI", i, i + 1), float(-HW), ALU.add)
+    quadsum("PZ", "PB", C("SCN", HW - 1, None, 0, 64, HW), C("SCN", HW - 1, None, 64, 128, HW), 6, lambda: tr(H("VALT"), bank(3, P, 0, 64)))
+    for k in range(6):
+        affine(C("AD", 32 * k, 32 * k + 32), C("SLT"), C("PZ", k, k + 1), -1.0, ACT.Abs)
+    for k in range(6):
+        affine(C("EV", 32 * k, 32 * k + 32), C("AD", 32 * k, 32 * k + 32), C("KEYC", k, k + 1), C("KEYN", k, k + 1), ACT.Relu)
+
+    def slots(v):
+        for k in range(6):
+            val = C("V2C", k, k + 1) if v == 1 else C("VALT", 32 * k, 32 * k + 1)
+            ts(C("EV", 192 * v + 32 * k, 192 * v + 32 * k + 32), C("SLT2" if v == 1 else "SLT"), C("PZ", k, k + 1), ALU.is_equal, val, ALU.mult)
+    slots(1)
+    tr(U("VALT"), bank(4, P, 64, 128))
+    tr(C("ET", 192, 384), C("EV", 192, 384))
+    slots(2)
+    tr(C("ET", 0, 192), C("EV", 0, 192))
+    tr(C("ET", 384, 576), C("EV", 384, 576))
+    total_of("s", H("land2", 380, 381), H("ET", 192, 384), H("J3", 192, 384))
+    total_of("s", U("land2", 382, 383), U("ET", 192, 384), U("J3", 192, 384))
+    copy("s", U("land2", 380, 381), H("land2", 380, 381))
+    copy("s", H("land2", 382, 383), U("land2", 382, 383))
+    for v, at in ((0, 3), (2, 1)):
+        pairsum((T.land2[:, at:384:4], "land2", 0, 128, 380 + at, 381 + at), C("ET", 192 * v, 192 * v + 96), C("ET", 192 * v + 96, 192 * v + 192))
+    fan(C("land2", 380, 384), "land2", 384, 4, "ar2")
+    arrive("ar2", arrivals(), [C("land2", 384, 412)])
+
+    iota(C("RA", e0 - 8, e0 + 232), [[0, 240]], 0, 0)
+    iota(C("RB", e0 - 8, e0 + 232), [[0, 240]], 0, 0)
+    iota(C("INI"), [[0, 1]], 0, 0)
+    iota(C("RA", e0 - 8, e0 + 232, 0, 16), [[0, 240]], -2, 0)
+    iota(C("INI", 0, 1, 0, 16), [[0, 1]], 320 - 2 * (E * r - ws - 1), 0)
+    for t, x in (("VA", 1), ("VB", 0)):
+        iota(H(t, 0, 32), [[0, 32]], -2 * Wn, 0)
+        iota(U(t, 0, 32), [[2 * G3 - 4 * Wn, 2], [0, 16]], -2 * G3 + 2 * x, 0)
+    iota(C("VA", 0, 32, 0, 16), [[0, 32]], -2 * Wn - 2, 0)
+    iota(H("SEC"), [[0, 32]], 0, 0)
+    iota(U("SEC"), [[0, 32]], 1, 0)
+    iota(C("ZT"), [[0, 32]], 0, 0)
+    for k in range(3):
+        iota(C("HT", k * Wn, k * Wn + Wn), [[4, Wn]], 4 * ws + 2 * (k // 2), 0)
+    iota(C("HT", G3, G3 + Wn), [[4, Wn]], 4 * ws + 1, 0)
+    ks, kn = (0, hL + hR) if hq == "HQ" else (0 if hL else Wn - 128, 128)
+    kids(hq, ks, kn, "FH1", "FH2", 5, "ssvsvssv")
+    affine(C("CT", 0, 16), C("CTI", 0, 16), C("CLM"), 1.0)
+    affine(C("CT", 16, 32), C("CTI", 16, 32), C("CLB"), 1.0)
+    quant("HK1", 0, kn, C("FH1", 0, 4 * kn))
+    quant("HK2", 0, kn, C("FH2", 0, 4 * kn))
+    if hq == "HQ":
+        move("W1", 0, "HQ", 0, hL)
+        move("W1", hL + P, "HQ", hL, hR)
+    for k in (1, 2):
+        move("W1", k * Wn, "HK%d" % k, 0, hL)
+        move("W1", k * Wn + hL + P, "HK%d" % k, kn - hR, hR)
+    move("W2", 0, "W1", 0, 3 * Wn)
+    move("W2", G3, "W1", 2 * Wn, Wn)
+    ts(C("OD"), C("OI2", 0, 20), PM16, ALU.add)
+    ts(C("OV"), C("OI2", 20, 22), IC, ALU.add)
+    quant("WQ", 0, 128, C("WB"))
+
+    for k in range(2):
+        total_of("s", C("VV", k + 2, k + 3), C("land2", 382 + k, 412, step=4), C("JJ", 8 * k, 8 * k + 8))
+        total_of("v", C("VV", k, k + 1), C("land2", 380 + k, 412, step=4))
+    for k in range(2):
+        ts(C("RBS", 32 * k, 32 * k + 32), C("C64"), 0.0, ALU.mult, C("VV", k, k + 1), ALU.add)
+        affine(C("RBK", 32 * k, 32 * k + 32), C("C64"), C("VV", k + 2, k + 3), 0.0)
+    affine(C("TK"), C("VV", 2, 3), 0.0, TAU)
+    affine(C("KB"), C("VV", 3, 4), -BIG, 1.0)
+    affine(C("NB"), C("VV", 2, 3), -BIG, 1.0)
+    tr(C("SC", 0, 64), C("RBS"))
+    tr(C("KY", 0, 64), C("RBK"))
+    swap("SC")
+    swap("KY")
+    pairs("SC", "vsvs")
+    pairs("KY", "vsvs")
+    affine(C("E1"), C("SC"), C("VV", 1, 2), -1.0)
+    ts(C("NK1"), C("KY"), C("VV", 3, 4), ALU.subtract, -TAU, ALU.mult)
+    affine(C("E2"), C("SC", 32, 192), C("VV", 0, 1), -1.0)
+    affine(C("NK2"), C("KY", 32, 192), C("TK"), -TAU)
+    tt(C("M1"), C("E1"), C("NK1"), ALU.is_lt)
+    tt(C("M2"), C("E2"), C("NK2"), ALU.is_lt)
+    pairsum(C("R1"), C("M1", 0, 96), C("M1", 96, 192))
+    pairsum(C("R2"), C("M2", 0, 80), C("M2", 80, 160))
+    R1, R2 = C("R1", 95, 96), C("R2", 79, 80)
+    gathered(C("GD"), C("KY"), C("OD", 4, 12), float(-ws), 0.5, ACT.Relu)
+    for f, a in ((H, 64), (U, 32)):
+        affine(f("FR", 192, 224), f("KY", a, a + 32), -BIG, 1.0)
+        affine(f("FR", 224, 256), f("KY", a + 96, a + 128), -BIG, 1.0)
+    affine(C("GE"), C("GD"), float(Wn - 1), -1.0, ACT.Relu)
+    affine(C("NKA"), C("VV", 2, 3), C("CN"), 1.0)
+    affine(C("Q1", 192, 256), C("FR", 192, 256), C("KB"), -1.0, ACT.Sign, C("S1A"))
+    affine(C("Q2", 192, 256), C("FR", 192, 256), C("NB"), -1.0, ACT.Sign, C("C2A"))
+    affine(C("KES"), C("VV", 3, 4), C("S1A"), 1.0)
+    affine(C("NKE"), C("NKA"), C("C2A"), 1.0)
+    for k in range(3):
+        affine(C("KE", k, k + 1), C("KES"), float(272 + 2 * k * DUMP), 1.0)
+    ts(C("FB", 32, 64), C("C64"), R1, ALU.is_gt, C("KB"), ALU.mult)
+    ts(C("FB", 0, 32), C("THT"), R2, ALU.is_gt, C("NB"), ALU.mult)
+    ts(C("FL"), C("C64", 0, 1), R1, ALU.is_gt)
+    ts(C("F2"), C("THT", 0, 1), R2, ALU.is_gt)
+    tr(C("FR", 0, 64), C("FB"))
+    tr(C("GT"), C("GE"))
+    swap("FR")
+    for k in (0, 1):
+        ts(C("OFFG", 4 * k, 4 * k + 4), C("GT", 0, 128, step=32), -1.0, ALU.mult, float((2 + k) * Wn - 1), ALU.add)
+    pairs("FR", "vsvs")
+    affine(C("Q1", 0, 192), C("FR", 0, 192), C("KB"), -1.0, ACT.Sign, C("S1"))
+    affine(C("Q2", 0, 192), C("FR", 0, 192), C("NB"), -1.0, ACT.Sign, C("C2"))
+    win, off, ct = C("KY", 0, 96), C("OV"), C("CT")
+    run("v", lambda: g.vector.tensor_tensor(T.VA[:, 32:64], win[0].indirect(off[0]), ct[0], ALU.subtract), [win, off, ct], [C("VA", 32, 64)])
+    for k, x in enumerate((2 * DUMP - 1, -2 * DUMP - 1, 1 - 4 * DUMP)):
+        ts(C("DB", k, k + 1), C("FL"), float(x), ALU.mult, C("KE", k, k + 1), ALU.add)
+    ts(C("DBN"), C("F2"), -6.0 * DUMP - 1, ALU.mult, C("NKE"), ALU.add)
+    tt(C("VB", 32, 64), C("VA", 32, 64), C("BLT"), ALU.add)
+    pick_codes("PK", 0, 128, "W1", 3 * Wn, C("OFFG"))
+    ts(C("OFF", 1, 4), C("DB"), C("S1"), ALU.add, 0.5, ALU.mult)
+    ts(C("OFF", 0, 1), C("C2"), C("DBN"), ALU.add, 0.5, ALU.mult)
+
+    scatter(C("RB"), C("OFF"), C("VB"))
+    scatter(C("RA"), C("OFF"), C("VA"))
+    affine(C("EB"), C("S1"), float(2 * e0 - 1), -1.0)
+    affine(C("BN"), C("DBN"), float(2 * e0 - 1), -1.0)
+    affine(C("JK", 0, 2), C("DB", 0, 2), C("EB"), -1.0, ACT.Sign, C("A12"))
+    affine(C("SGN"), C("C2"), C("BN"), -1.0, ACT.Sign)
+    affine(C("SB1"), C("DB", 2, 3), C("EB"), -1.0, ACT.Sign)
+    affine(C("AN"), C("SGN"), C("A12"), 1.0)
+    pick_scales("PK", 0, 128, "W1", 3 * Wn, C("OFFG"))
+    scaled("s", C("RB", e0 - 1, e0), C("RB", e0 - 1, e0), 0.0)
+    affine(C("XS", 224, 256), C("SEC"), C("SB1"), C("AN"))
+    xa, xb, x0, xo = C("RA", e0, e0 + 224), C("RB", e0 - 1, e0 + 223), C("INI"), C("XS", 0, 224)
+    run("v", lambda: g.vector.tensor_tensor_scan(xo[0], xa[0], xb[0], x0[0], ALU.add, ALU.subtract), [xa, xb, x0], [xo])
+    tr(C("XT"), C("XS"))
+    gathered(C("HT", G1, G1 + 128), C("KY"), C("OD", 12, 20), 0.0, 2.0, ACT.Identity)
+    total_of("s", C("ZS", 7, 8), C("XT", 224, 256), C("J3", 0, 32))
+    tt(C("ZS", 0, 7), C("XT", 0, 224, step=32), C("XT", 16, 224, step=32), ALU.add)
+    kids("PK", 0, 128, "GH1", "GH2", 5, "ssssssss")
+    quadsum("ZT", "HS", H("ZS"), U("ZS"), 8)
+    tr(C("XR"), C("ZT"))
+    quant("W2", G1, G1 + 128, C("GH1"))
+    gather("v", C("YY"), C("XR"), C("OD", 0, 4))
+    tr(C("YT"), C("YY"))
+    quant("W2", G2, G2 + 128, C("GH2"))
+    for h in (0, 1):
+        ts(part_of("OFFL", h, 14, 2), C("YT", 32 * h, 32 * h + 7), C("ZT", 7, 8), ALU.add, -0.5, ALU.mult)
+    affine(C("HT", G2, G2 + 128), C("HT", G1, G1 + 128), 1.0, 1.0)
+    for c0, c1 in ((0, 128), (128, E)):
+        off = C("OFFL", c0 // 16, c1 // 16)
+        pick_codes("FQ", c0, c1, "W2", G3 + Wn, off)
+        pick_scales("FQ", c0, c1, "W2", G3 + Wn, off)
+    mm(bank(0, 128), "WQ", 0, "FQ", 0, 128)
+    mm(bank(1, 128), "WQ", 0, "FQ", E - 128, E)
+    dma("y", ext(T.oc[:, :]), C("FQ"), bits=2)
+    gather("s", C("HR"), C("HT", 0, G3 + Wn), C("OFFL", 0, 13))
+    for k in range(4):
+        dma("yyss"[k], ext(T.osc[4 * k:4 * k + 4, :]), C("FQS", 0, E, 32 * k, 32 * k + 4))
+    copy("v", C("YS", 0, 128), bank(0, 128))
+    dma("y", ext(T.y[:, 0:128]), C("YS", 0, 128))
+    copy("v", C("YS", 128, E), bank(1, 128, 0, 128, 256 - E))
+    dma("y", ext(T.y[:, 128:E]), C("YS", 128, E))
+    dma("s", ext(T.hs[:, :]), C("HR", 0, E, 0, 1))
+
+    total["loc"] = loc[0]
+    for sem in SEMAPHORES:
+        if total.get(sem):
+            need("g", sem, total[sem], {})

@@ -6,18 +6,18 @@ ACT = ActivationFunctionType
 N, P, K, E = 8, 192, 64, 208
 WMAX = 336
 TAU = 2.0 ** -106
+EPS = 2.0 ** -13
 BIG = 65536.0
 DUMP = 1720
-ROW = 8 + 4 * DUMP
-CW = 416
+ROW = 8 + 2 * DUMP
+CW = 352
 HW = CW // 2
-NV = 4
+LOW = 256
 
 SMALL = {}
-for _n, _w in dict(PB=6, PZ=6, LO=2, HI=2, QOB=1, NST=2, RK=6, KEYC=6, KEYN=6, V2C=6, VV=4, FL=1, F2=1, TH=1, KB=1, NB=1, TK=1,
-                   PID=1, BITS=4, SG=1, ISC=1, CK=1, I2=1, NT=1, NTB=1, NTN=6, S1A=1, C2A=1, KES=1, KE=3, DB=3, DBN=1, NKA=1, NKE=1,
-                   CN=1, BN=1, EB=1, S1=1, C2=1, A12=1, SB1=1, SGN=1, AN=1, INI=1, CLA=1, CLP=1, CLM=1, CLB=1, BL1=1, BL2=1, GRP=1,
-                   GR=1, ZS=8, HS=8, JJ=16, JK=8).items():
+for _n, _w in dict(PB=6, PZ=6, LO=2, HI=2, NST=2, LS=2, LM=2, LAM=6, PINF=6, BITS=5, MQ=4, ISC=1, U4F=4, QS2=1, KB0=1, CA=1, CK=1,
+                   GB=1, MB=1, Y0=1, YB=1, YC=1, YD=1, AM=1, AM2=1, BM=1, DT=1, DL=1, CB0=1, CB=1, TK=1, KB=2, KBH=2, TA=2, SA=2,
+                   KC=2, KK=6, KEP=2, GG=2, SB=2, EB=2, AA=2, INI=1, ZS=64, HS=16, JK=8, BIT2=2, LF=2).items():
     SMALL[_n] = (8 * sum((w + 7) // 8 for _, w in SMALL.values()), _w)
 
 
@@ -28,18 +28,17 @@ def _scratch():
     def sb(dtype, **kw):
         for name, n in kw.items():
             d[name] = ("sbuf", [128, n], dtype)
-    sb(h, XB=4 * P, U4=4, UB=512, AB=2048, BB=2048, WB=512, KH1=4 * P, KH2=4 * P, FH1=576, FH2=576,
-       GH1=512, GH2=512, CM=6 * CW, SCN=6 * HW, J1=2 * CW, M1=192, M2=160, Z0=128)
-    for name, n in dict(UQ=128, AQ=512, BQ=512, WQ=128, W1=3 * WMAX, HQ=144, HK1=144, HK2=144, PK=128, W2=4 * WMAX + 256, FQ=E).items():
+    sb(h, XB=4 * P, U4=4, UB=2048, AB=2048, BB=2048, WB=512, KH1=4 * P, KH2=4 * P, FH1=576, FH2=576, GH1=512, GH2=512,
+       CM=6 * CW, SCN=4 * HW, J1=2 * CW, MA=384, Z0=128, PMR=192, E1=384, KD=384, M1=384, JA=128, JB=384)
+    for name, n in dict(HX=128, UQ=512, AQ=512, BQ=512, WQ=128, W1=3 * WMAX, HQ=144, HK1=144, HK2=144, PK=128, W2=4 * WMAX + 256, FQ=E).items():
         d[name] = ("sbuf", [128, n], q)
         d[name + "S"] = ("sbuf", [128, n], s)
-    sb(f, BLT=32, C64=32, THT=32, OC=8, OCB=64, TOWN=64, ST0=192, DL=384, TI0=64, TIE=384, land1=24, LB=352, LT=352,
-       SLT=32, SLT2=32, VALT=192, AD=192, EV=576, ET=576, land2=412, RBS=64, RBK=64, SC=192, KY=192, E1=192, E2=160, NK1=192,
-       NK2=160, R1=96, R2=80, FB=64, FR=256, Q1=256, Q2=256, VA=64, VB=64, CTI=32, CT=32, SEC=32, RA=ROW, RB=ROW, XS=256, XT=256,
-       ZT=32, XR=32, YY=64, YT=64, HT=4 * WMAX + 256, HR=E, GD=128, GE=128, GT=128, YS=E, J3=416, OI2=22,
+    sb(f, C64=32, ONE=32, ZF=40, OC=8, ST0=192, TI=256, TIE=256, LA=192, land1=24, LB=352, LT=352, VROW=192, VAL=96, RS=1600, ET=128,
+       land2=160, RBS=72, RBK=72, SC=192, KY=200, FB=64, FR=192, VA=64, V2=32, XY=32, WW=32, CTI=32, CT=32, RA=ROW, MSK=224, M4=60, RR=192,
+       XS=272, XT=480, ZT=32, HT=4 * WMAX + 256, HR=E, GD=128, GE=128, GT=128, YS=E, J3=32, OI2=8,
        SM=8 * sum((w + 7) // 8 for _, w in SMALL.values()))
-    sb("int32", OI=26, PIN=1, PA=4)
-    sb("uint16", OU=26, OD=20, OV=2, OFF=4, OFFG=8, OFFL=14)
+    sb("int32", OI=24, PIN=6, PA=7)
+    sb("uint16", OU=22, OFV=6, OFZ=6, OVK=2, OD=8, OFF=4, OFFG=8, OFFL=16, OLF=2)
     d["PS"] = ("psum", [128, 4096], f)
     return d
 
@@ -82,18 +81,21 @@ def rank_program(g, core, T, topo):
         ap = T[name][p0:p1, c0:c1] if step == 1 else T[name][p0:p1, c0:c1:step]
         return (ap, name, p0, p1, c0, c1)
 
-    def H(name, c0=0, c1=None):
-        return C(name, c0, c1, 0, 64)
+    def H(name, c0=0, c1=None, step=1):
+        return C(name, c0, c1, 0, 64, step)
 
-    def U(name, c0=0, c1=None):
-        return C(name, c0, c1, 64, 128)
+    def U(name, c0=0, c1=None, step=1):
+        return C(name, c0, c1, 64, 128, step)
 
-    def Q(name, q, c0=0, c1=None):
-        return C(name, c0, c1, 32 * q, 32 * q + 32)
+    def Q(name, q, c0=0, c1=None, step=1):
+        return C(name, c0, c1, 32 * q, 32 * q + 32, step)
 
-    def part_of(name, i, n, step):
+    def R3(name, c0=0, c1=None, step=1):
+        return C(name, c0, c1, 0, 96, step)
+
+    def part_of(name, i, n, step, c0=0):
         w = n // step
-        return (T[name][:, i:n:step], name, 0, 128, i * w, i * w + w)
+        return (T[name][:, c0 + i:c0 + n:step], name, 0, 128, c0 + i * w, c0 + i * w + w)
 
     def bank(k, n, p0=0, p1=128, c0=0):
         return (T.PS[p0:p1, 512 * k + c0:512 * k + n], "PS", 0, 128, 512 * k, 512 * k + 512)
@@ -175,17 +177,20 @@ def rank_program(g, core, T, topo):
     def tt(o, a, b, op):
         run("v", lambda: g.vector.tensor_tensor(o[0], a[0], b[0], op), [a, b], [o])
 
+    def tt_by(o, win, off, b, op):
+        src = win[0].indirect(off[0])
+        run("v", lambda: g.vector.tensor_tensor(o[0], src, b[0], op), [win, off, b], [o])
+
     def tr(o, i):
         run("v", lambda: g.vector.transpose(o[0], i[0]), [i], [o])
 
-    def total_of(q, o, i, junk=None):
-        if q == "v":
-            run("v", lambda: g.vector.tensor_reduce(o[0], i[0], AxisListType.X, ALU.add), [i], [o])
-        else:
-            run("s", lambda: g.scalar.activation(junk[0], i[0], ACT.Copy, accum_out=o[0]), [i], [o, junk])
+    def total_of(o, i, junk):
+        run("s", lambda: g.scalar.activation(junk[0], i[0], ACT.Copy, accum_out=o[0]), [i], [o, junk])
 
     def pairsum(o, a, b, start=0.0):
-        run("v", lambda: g.vector.tensor_tensor_scan(o[0], a[0], b[0], start, ALU.add, ALU.add), [a, b], [o])
+        s = start[0] if isinstance(start, tuple) else start
+        run("v", lambda: g.vector.tensor_tensor_scan(o[0], a[0], b[0], s, ALU.add, ALU.add),
+            [a, b] + ([start] if isinstance(start, tuple) else []), [o])
 
     def affine(o, i, bias, scale, func=ACT.Identity, acc=None):
         rd = [i] + [x for x in (bias, scale) if isinstance(x, tuple)]
@@ -202,7 +207,7 @@ def rank_program(g, core, T, topo):
 
     def gathered(o, win, off, bias, scale, func):
         src = win[0].indirect(off[0])
-        run("s", lambda: g.scalar.activation(o[0], src, func, bias=bias, scale=scale), [win, off], [o])
+        run("s", lambda: g.scalar.activation(o[0], src, func, bias=bias[0], scale=scale), [win, off, bias], [o])
 
     def scatter(win, off, i):
         run("v", lambda: g.vector.tensor_copy(win[0].indirect(off[0]), i[0]), [i, off], [win])
@@ -211,9 +216,20 @@ def rank_program(g, core, T, topo):
         o, s = C(name, c0, c1), C(name + "S", c0, c1)
         run("v", lambda: g.vector.quantize_mx(o[0], s[0], src[0]), [src], [o, s])
 
-    def mm(o, l, lc, x, x0, x1):
-        a, b, c, d = C(l, lc, lc + 128), C(l + "S", lc, lc + 128), C(x, x0, x1), C(x + "S", x0, x1)
-        run("t", lambda: g.tensor.matmul_mx(o[0], a[0], b[0], c[0], d[0], True, True), [a, b, c, d], [o])
+    def sides(l, lc, x, x0, x1):
+        return [C(l, lc, lc + 128), C(l + "S", lc, lc + 128), C(x, x0, x1), C(x + "S", x0, x1)]
+
+    def mm(o, *args):
+        v = sides(*args)
+        run("t", lambda: g.tensor.matmul_mx(o[0], v[0][0], v[1][0], v[2][0], v[3][0], True, True), v, [o])
+
+    def mm2(o, first, second):
+        v, w = sides(*first), sides(*second)
+
+        def both():
+            g.tensor.matmul_mx(o[0], v[0][0], v[1][0], v[2][0], v[3][0], True, False)
+            return g.tensor.matmul_mx(o[0], w[0][0], w[1][0], w[2][0], w[3][0], False, True)
+        run("t", both, v + w, [o])
 
     part = [False]
 
@@ -232,27 +248,19 @@ def rank_program(g, core, T, topo):
     def pick_scales(o, c0, c1, src, n, off):
         gather("s", C(o + "S", c0, c1), C(src + "S", 0, n), off)
 
-    def quadsum(o, h, lo, up, n, between=None):
+    def quadsum(o, h, lo, up, n):
         tt(H(h, 0, n), lo, up, ALU.add)
-        if between:
-            between()
         for q in range(4):
             tt(Q(o, q, 0, n), Q(h, 0, 0, n), Q(h, 1, 0, n), ALU.add)
 
-    def swap(name):
-        copy("s", H(name, 64, 96), U(name, 32, 64))
-        copy("v", U(name, 64, 96), H(name, 32, 64))
+    def spread(name, order):
+        for k, (to, at, of) in enumerate(((0, 1, 1), (1, 1, 0), (2, 1, 0), (0, 2, 2), (1, 2, 2), (2, 2, 1))):
+            copy(order[k], Q(name, to, 64 * at, 64 * at + 64), Q(name, of, 0, 64))
 
-    def pairs(name, order):
-        for q in range(4):
-            copy(order[q], Q(name, q, 96, 192), Q(name, q ^ 1, 0, 96))
-
-    def kids(src, c0, n, t1, t2, first, pat, late=None):
-        for i in range(8):
-            k = (first + i) % 8
+    def kids(src, c0, n, t1, t2, banks, pat, steps=range(8)):
+        for i in steps:
+            k = banks[i % len(banks)]
             mm(bank(k, n), "AQ" if i < 4 else "BQ", 128 * (i % 4), src, c0, c0 + n)
-            if i == 7 and late:
-                late()
             scaled(pat[i], part_of(t1 if i < 4 else t2, i % 4, 4 * n, 4), bank(k, n), 0.0625)
 
     def ways(a):
@@ -266,7 +274,7 @@ def rank_program(g, core, T, topo):
     def arrivals():
         return sum(len(split(c, core)) for c in T.cores if c != core)
 
-    def fan(src, dst, base, width, arr):
+    def fan(src, dst, width, arr):
         deps("g", [src], [])
         others = [c for c in T.cores if c != core]
         far = [c for c in others if topo.chip(c) != topo.chip(core)]
@@ -274,14 +282,12 @@ def rank_program(g, core, T, topo):
         fe, ne = split(core, far[0]), split(core, near[0])
 
         def tf(dsts, eng):
-            ids, aps = [], []
+            ids = []
             for c in dsts:
-                d = T.rank_of(c)
-                k = base + width * (r if r < d else r - 1)
                 rid, pid, _ = topo.addr(c)
                 ids.append(DstId(rid=rid, pnc=pid))
-                aps.append(T[dst][:, k:k + width])
-            return RemoteDMATransfer(dst_ids=ids, dma_engine_mask=sum(1 << e for e in eng), remote_sem=T.sem[arr], srcs=[src[0]], dsts=aps)
+            return RemoteDMATransfer(dst_ids=ids, dma_engine_mask=sum(1 << e for e in eng), remote_sem=T.sem[arr], srcs=[src[0]],
+                                     dsts=[T[dst][:, width * r:width * r + width] for _ in dsts])
         g.remote_dma_fused([tf(far, fe), tf(near, ne)], local_sem=T.sem.loc)
         loc[0] += len(fe) + len(ne)
 
@@ -290,7 +296,7 @@ def rank_program(g, core, T, topo):
         dst, a, b = _land(d)
         c0, c1, at = (P - _halo(d)[0], P, a) if d > r else (0, _halo(d)[1], b)
         rid, pid, _ = topo.addr(c)
-        s = C("W1" + sfx, hL + c0, hL + c1)
+        s = C("HX" + sfx, c0 - hx, c1 - hx) if d == early else C("W1" + sfx, hL + c0, hL + c1)
         deps("g", [s], [])
         o, i = T[dst + sfx][:, at:at + c1 - c0], s[0]
         if not sfx:
@@ -300,202 +306,219 @@ def rank_program(g, core, T, topo):
 
     def arrive(sem, val, writes):
         for _, name, p0, p1, c0, c1 in writes:
-            recs.setdefault(name, []).append((p0, p1, c0, c1, True, "far", sem, val, {sem: val}))
+            if c1 > c0:
+                recs.setdefault(name, []).append((p0, p1, c0, c1, True, "far", sem, val, {sem: val}))
         total[sem] = val
 
     dma("s", C("U4"), ext(T.u[:, 0:4]))
-    for name, t in (("XB", T.x), ("AB", T.a), ("BB", T.b), ("WB", T.w)):
+    early = r - 1 if r else r + 1
+    hx = 0 if r else P - 128
+    for c0, c1 in ((hx, hx + 128), (128, P) if r else (0, hx)):
+        dma("y", C("XB", 4 * c0, 4 * c1), ext(T.x[:, 4 * c0:4 * c1]))
+    for name, t in (("AB", T.a), ("BB", T.b)):
         dma("y", C(name), ext(t[:, :]))
 
-    iota(C("PIN"), [[0, 1]], 0, 1, True)
-    iota(C("RK"), [[64, 6]], 2 * P * r, 0)
-    iota(C("TI0"), [[64, 2], [1, 32]], 0, 0)
-    iota(C("OI", 0, 2), [[0, 2]], 0, 0, True)
-    iota(C("OI", 2, 4), [[0, 2]], 4, 0, True)
-    upper = [(2, 4, -3)]
-    at, nb, na = 4, r, N - 1 - r
-    for what, s0, n in (("main", 0, nb), ("rest", 0, nb), ("rest", nb, na), ("main", nb, na)):
-        if what == "main" and n:
-            iota(C("OI", at, at + 2 * n), [[2, n], [0, 2]], 2 * s0, 0, True)
-            at += 2 * n
-        elif n:
-            m = (n + 1) // 2
-            iota(C("OI", at, at + 2 * m), [[4, m], [0, 2]], 2 * s0 + 1, 0, True)
-            if n // 2:
-                upper.append((at, at + 2 * (n // 2), 2))
-            if n % 2:
-                upper.append((at + n - 1, at + n + 1, 16 - (2 * s0 + 1 + 4 * (m - 1))))
-            at += 2 * m
-    cut = 32 * (nb + (nb + 1) // 2)
+    iota(C("PIN"), [[32, 6]], 0, 1, True)
+    iota(C("TI"), [[-1, 256]], 64, 1)
+    iota(C("OI"), [[4, 4], [1, 3], [0, 2]], 0, 0, True)
+    odd, pair = r % 2, r // 2
+    skip = 6 * pair + 4 * odd
+    cut = 32 * (3 * pair + 2 * odd)
+    vb, sb_ = (2, 0) if odd else (0, 4)
     memset(C("Z0"), 0.0)
-    memset(C("OC"), -9e29)
-    memset(C("land1", 16, 20), -9e29)
-    memset(C("C64"), 64.0)
-    copy("v", C("PID"), C("PIN"))
-    for k, m in enumerate((31, 15, 32, 112)):
-        ts(C("PA", k, k + 1), C("PIN"), m, ALU.bitwise_and)
-    copy("v", C("BITS"), C("PA"))
-    IC, PM16, QO, GR = [C("BITS", k, k + 1) for k in range(4)]
-    affine(C("SG"), C("PID"), -63.5, 1.0, ACT.Sign)
-    affine(C("I2"), IC, 0.0, 2.0)
-    affine(C("TH"), IC, 64.0, -1.0)
-    affine(C("GR"), GR, 0.0, 1.0, ACT.Sign)
-    affine(C("QOB"), QO, float(-4 * HW), 1.0)
-    affine(C("ISC"), C("SG"), 0.0, 1.0, ACT.Relu)
-    affine(C("NT"), C("PID"), C("I2"), -1.0)
-    affine(C("CLA"), PM16, C("PID"), -1.0)
-    affine(C("GRP"), C("GR"), 2.0, -2.0)
-    affine(C("SLT"), C("TI0", 0, 32), C("QOB"), 1.0)
-    affine(C("CK"), C("I2"), C("ISC"), 1.0)
-    affine(C("NTB"), C("NT"), P * r * TAU, -TAU)
-    affine(C("THT"), C("TI0", 0, 32), C("TH"), 0.0)
-    affine(C("SLT2"), C("SLT"), 64.0, 1.0)
-    affine(C("NTN"), C("RK"), C("NTB"), -0.5 * TAU)
-    affine(C("KEYC"), C("RK"), C("CK"), 1.0)
-    affine(U("V2C"), U("RK"), U("I2"), 1.0)
-    affine(C("CLP"), C("CLA"), C("GRP"), 2.0)
-    affine(C("KEYN"), C("KEYC"), 0.0, -1.0)
+    memset(C("PMR", 0, 64), 1.0)
+    memset(C("PMR", 64, 192), -1.0)
+    copy("v", C("PINF"), C("PIN"))
+    PID = C("PINF", 0, 1)
+    for k, m in enumerate((96, 15, 32, 16, 8)):
+        ts(C("PA", k, k + 1), C("PIN", 0, 1), m, ALU.bitwise_and)
+    copy("v", C("BITS"), C("PA", 0, 5))
+    QO, PM16, B32, B16, B8 = [C("BITS", k, k + 1) for k in range(5)]
+    M0, M1 = C("MQ", 0, 1), C("MQ", 1, 2)
+    for c in (1280, 1408, 1664, 1792, 1920):
+        copy("s", C("UB", c, c + 128), C("Z0"))
+    copy("s", C("U4F"), C("U4"))
+    for t in range(4):
+        affine(part_of("UB", t, 768, 4, 512), C("PMR"), 0.0, C("U4F", t, t + 1), ACT.Copy)
+    scaled("s", C("TIE"), C("TI"), TAU)
 
     for t in range(4):
         ts(part_of("UB", t, 512, 4), C("Z0"), C("U4", t, t + 1), ALU.add)
-    quant("UQ", 0, 128, C("UB"))
+    quant("HX", 0, 128, C("XB", 4 * hx, 4 * hx + 512))
+    quant("UQ", 0, 128, C("UB", 0, 512))
     quant("W1", hL, hL + P, C("XB"))
     pieces = [(d, sfx) for sfx in ("S", "") for d in (r - 1, r + 1) if 0 <= d < N]
     halo(*pieces[0])
-    mm(bank(1, 128), "W1", hL, "UQ", 0, 128)
-    mm(bank(2, 128), "W1", hL + 64, "UQ", 0, 128)
+    mm(bank(1 if r else 2, 128), "HX", 0, "UQ", 0, 128)
+    mm(bank(2 if r else 1, 128), "W1", hL + 64 - hx, "UQ", 0, 128)
     mm(bank(0, P), "UQ", 0, "W1", hL, hL + P)
-    copy("v", C("OC", 0, 1), bank(1, 1))
-    copy("v", U("OC", 1, 2), bank(2, 1, 64, 128))
-    copy("v", H("OC", 1, 2), bank(2, 1, 64, 128))
-    fan(C("OC", 0, 2), "land1", 0, 2, "ar1")
-    arrive("ar1", arrivals(), [C("land1", 0, 14)])
+    ts(C("ISC"), PID, 64.0, ALU.is_ge)
+    quant("UQ", 128, 320, C("UB", 512, 1280))
+    for k, c in ((3, 0), (4, 64)):
+        mm2(bank(k, P), ("W1", hL + c, "UQ", 0, P), ("UQ", P, "W1", hL, hL + P))
+    copy("s" if r else "v", C("OC", 0, 1), bank(1, 1))
+    copy("v" if r else "s", C("OC", 1, 2), bank(2, 1))
+    ts(C("MQ"), C("PINF", 0, 4), PID, ALU.subtract, QO, ALU.is_equal)
+    ts(C("OFV"), C("PINF"), QO, ALU.subtract)
+    for c0, c1, x in ((0, skip, 0), (skip, 22, 2)):
+        if c1 > c0:
+            ts(C("OU", c0, c1), C("OI", c0 + x, c1 + x), C("ISC"), ALU.add)
+    memset(U("OU", skip - 2, skip) if odd else H("OU", skip, skip + 2), 16)
+    fan(C("OC", 0, 2), "land1", 2, "ar1")
+    arrive("ar1", arrivals(), [C("land1", 0, 16)])
     for piece in pieces[1:]:
         halo(*piece)
     want = sum(2 * len(ways(T.cores[d])) for d in (r - 1, r + 1) if 0 <= d < N)
     hq, hl, hr = _land(r)
-    arrive("arh", want, [C(hq + x, a, b) for x in ("", "S") for a, b in ((hl, hl + hL), (hr, hr + hR)) if b > a])
-    iota(C("OI2", 0, 4), [[16, 2], [0, 2]], 0, 0)
-    iota(C("OI2", 20, 22), [[0, 2]], 32, 0)
-    iota(C("CTI"), [[2 * (G2 - G1) - 2, 2], [2, 16]], 2 * (G1 + ws), 0)
-    for q in range(4):
-        st, sh = (96 if q % 2 == 0 else -96), (32 if q < 2 else -32)
-        iota(Q("OI2", q, 4, 12), [[st, 2], [16, 2], [0, 2]], 96 * (q % 2) + 32 + 32 * (q // 2), 0)
-        iota(Q("OI2", q, 12, 20), [[sh, 2], [st, 2], [16, 2]], 96 * (q % 2) + 32 + 32 * (q // 2), 0)
+    arrive("arh", want, [C(hq + x, a, b) for x in ("", "S") for a, b in ((hl, hl + hL), (hr, hr + hR))])
 
-    copy("v", C("OU"), C("OI"))
-    for c0, c1, x in upper:
-        ts(U("OU", c0, c1), U("OI", c0, c1), float(x), ALU.add)
-    gather("s", C("OCB"), C("OC"), C("OU", 0, 4))
+    def fill(o, val):
+        iota(o, [[0, o[5] - o[4]]], val, 0)
+    iota(C("OI2"), [[16, 4], [0, 2]], 0, 0)
+    iota(C("CTI"), [[64, 2], [2, 16]], 2 * (G2 + ws), 0)
+    fill(C("land2", 32, 160), 0)
+    fill(C("ZF"), 0)
+    fill(C("C64"), 64)
+    fill(C("KY", 192, 200), 0)
+
     tr(C("ST0"), bank(0, P))
-    for k in range(6):
-        affine(C("TIE", 64 * k, 64 * k + 64), C("TI0"), C("NTN", k, k + 1), TAU)
-    tr(C("TOWN"), C("OCB"))
-    quant("AQ", 0, 512, C("AB"))
-    for k in range(6):
-        ts(C("DL", 64 * k, 64 * k + 64), C("TOWN"), C("ST0", 32 * k, 32 * k + 1), ALU.subtract)
-    for k in range(6):
-        tt(C("CM", CW * k + 352, CW * k + CW), C("DL", 64 * k, 64 * k + 64), C("TIE", 64 * k, 64 * k + 64), ALU.is_gt)
-    quant("BQ", 0, 512, C("BB"))
-    copy("s", H("V2C"), C("ST0", 0, 192, 0, 64, 32))
-    affine(C("CLB"), C("ISC"), C("CLP"), 1.0)
-    affine(C("CLM"), C("ISC"), C("CLP"), -1.0)
-    affine(C("CN"), C("ISC"), float(272 + 6 * DUMP), 2.0)
-    affine(C("BL1"), C("ISC"), C("GRP"), -2.0)
-    affine(C("BL2"), C("GRP"), -2.0, 1.0)
-    for k in range(NV, 6):
-        scaled("s", C("NST", k - NV, k - NV + 1), C("ST0", 32 * k, 32 * k + 1), -1.0)
-    affine(C("BLT", 0, 16), C("TI0", 0, 16), C("BL1"), 0.0)
-    affine(C("BLT", 16, 32), C("TI0", 0, 16), C("BL2"), 0.0)
+    memset(C("land1", 16, 20), -9e29)
+    for t in range(4):
+        affine(part_of("UB", t, 128, 4, 1536), C("PMR", 0, 32), 0.0, C("U4F", t, t + 1), ACT.Copy)
+    affine(C("QS2"), B32, float(4 * LOW), 2.0)
+    affine(C("KB0"), PID, float(2 * P * r), 2.0)
+    for k in range(2):
+        scaled("s", C("NST", k, k + 1), C("ST0", 32 * (sb_ + k), 32 * (sb_ + k) + 1), -1.0)
+    affine(Q("VROW", 3), Q("TI", 3, 64, 256), Q("KB0", 3), -2.0)
+    copy("s", C("RS", 64, 192), C("Z0"))
+    copy("s", C("land2", 4 * r, 4 * r + 4), C("Z0", 0, 4))
+    for c in (0, 256):
+        quant("AQ", c, c + 256, C("AB", 4 * c, 4 * c + 1024))
+    tt(C("MA", 0, P), bank(3, P), C("TIE", 64, 256), ALU.is_lt)
+    tt(C("MA", P, 2 * P), bank(4, P), C("TIE", 0, P), ALU.is_lt)
+    kids("W1", hL, P, "KH1", "KH2", (5, 6, 7, 1, 2), "ssssssss", range(4))
+    for c in (0, 256):
+        quant("BQ", c, c + 256, C("BB", 4 * c, 4 * c + 1024))
+    for k in range(2):
+        pairsum(C("LA", 96 * k, 96 * k + 96), C("MA", P * k, P * k + 96), C("MA", P * k + 96, P * k + P))
+    quant("UQ", 320, 512, C("UB", 1280, 2048))
+    kids("W1", hL, P, "KH1", "KH2", (5, 6, 7, 1, 2), "ssssssss", range(4, 8))
 
-    def last(k):
-        return C("SCN", HW * k + HW - 1, HW * k + HW)
+    def field(q, c, start, stop):
+        v = sides("UQ", 384 - 32 * q, "W1", c, c + P)
+        run("t", lambda: g.tensor.matmul_mx(bank(0, P)[0], v[0][0], v[1][0], v[2][0], v[3][0], start, stop), v, [bank(0, P)])
+    for k in range(3):
+        src, q0 = ((0, 0), (0, 2) if odd else (1, 0), (1, 2))[k]
+        affine(C("LAM", 2 * k, 2 * k + 2), C("MQ", q0, q0 + 2), float((cut if 2 * k == sb_ else 0) - LOW), C("LA", 96 * src + 95, 96 * src + 96))
 
     def tally(k):
-        pairsum(C("SCN", HW * k, HW * k + HW), C("CM", CW * k, CW * k + HW), C("CM", CW * k + HW, CW * k + CW), float(-HW))
+        i = k - vb
+        pairsum(C("SCN", HW * i, HW * i + HW), C("CM", CW * k, CW * k + HW), C("CM", CW * k + HW, CW * k + CW), C("LAM", k, k + 1))
 
     def against(k):
         sc = C("ST0", 32 * k, 32 * k + 1)
         if cut > 0:
             ts(C("CM", CW * k, CW * k + cut), C("LT", 0, cut), sc, ALU.is_ge)
-        if cut < 352:
-            ts(C("CM", CW * k + cut, CW * k + 352), C("LT", cut, 352), sc, ALU.is_gt)
+        if cut < CW:
+            ts(C("CM", CW * k + cut, CW * k + CW), C("LT", cut, CW), sc, ALU.is_gt)
 
-    def signs(k):
-        c, i, j = CW * k, k - NV, CW * (k - NV)
-        affine(C("CM", c, c + 352), C("LT"), C("NST", i, i + 1), 1.0, ACT.Sign)
-        if cut > 0:
+    def signs():
+        lam = [C("LAM", sb_ + i, sb_ + i + 1) for i in range(2)]
+        for i in range(2):
+            affine(C("CM", CW * (sb_ + i), CW * (sb_ + i + 1)), C("LT"), C("NST", i, i + 1), 1.0, ACT.Sign)
+        for i in range(2 if cut > 0 else 0):
+            c, j = CW * (sb_ + i), CW * i
             affine(C("J1", j, j + cut), C("CM", c, c + cut), 0.0, -1.0, ACT.Relu, C("LO", i, i + 1))
-        affine(C("J1", j + cut, j + CW), C("CM", c + cut, c + CW), 0.0, 1.0, ACT.Relu, C("HI", i, i + 1))
+        for i in range(2 if cut < CW else 0):
+            c, j = CW * (sb_ + i), CW * i
+            affine(C("J1", j + cut, j + CW), C("CM", c + cut, c + CW), 0.0, 1.0, ACT.Relu, C("HI", i, i + 1))
+            if i == 0 and cut > 0:
+                for k in range(2):
+                    affine(C("LM", k, k + 1), C("LO", k, k + 1), lam[k], -1.0)
+                lam = [C("LM", k, k + 1) for k in range(2)]
+        for i in range(2):
+            if cut < CW:
+                affine(C("LS", i, i + 1), C("HI", i, i + 1), lam[i], 1.0)
+            else:
+                affine(C("LS", i, i + 1), C("LO", i, i + 1), lam[i], -1.0)
 
-    kids("W1", hL, P, "KH1", "KH2", 3, "ssssssss", lambda: gather("s", C("LB", 192, 352), C("land1", 0, 20), C("OU", 16, 26)))
+    field(2, hL, True, False)
     quant("W1", Wn + hL, Wn + hL + P, C("KH1"))
-    gather("v", C("LB", 0, 192), C("land1", 0, 20), C("OU", 4, 16))
-    tr(C("LT", 0, 192), C("LB", 0, 192))
-    tr(C("LT", 192, 352), C("LB", 192, 352))
-    mm(bank(3, P), "UQ", 0, "W1", Wn + hL, Wn + hL + P)
-    signs(4)
-    signs(5)
-    against(0)
-    against(1)
-    tally(0)
+    field(0, Wn + hL, False, False)
+    for k, (x, y) in enumerate(((1, 0), (15, 1))):
+        ts(C("PA", 5 + k, 6 + k), C("PIN", 0, 1), x, ALU.bitwise_and, y, ALU.logical_shift_right)
     quant("W1", 2 * Wn + hL, 2 * Wn + hL + P, C("KH2"))
-    mm(bank(4, P), "UQ", 0, "W1", 2 * Wn + hL, 2 * Wn + hL + P)
-    against(2)
-    tally(1)
-    against(3)
-    tally(2)
-    tally(3)
-    for k in range(NV, 6):
-        i = k - NV
-        if cut > 0:
-            ts(last(k), C("HI", i, i + 1), C("LO", i, i + 1), ALU.subtract, float(cut - HW), ALU.add)
-        else:
-            ts(last(k), C("HI", i, i + 1), float(-HW), ALU.add)
-    quadsum("PZ", "PB", C("SCN", HW - 1, None, 0, 64, HW), C("SCN", HW - 1, None, 64, 128, HW), 6, lambda: tr(H("VALT"), bank(3, P, 0, 64)))
-    for k in range(6):
-        affine(C("AD", 32 * k, 32 * k + 32), C("SLT"), C("PZ", k, k + 1), -1.0, ACT.Abs)
-    for k in range(6):
-        affine(C("EV", 32 * k, 32 * k + 32), C("AD", 32 * k, 32 * k + 32), C("KEYC", k, k + 1), C("KEYN", k, k + 1), ACT.Relu)
+    field(1, 2 * Wn + hL, False, True)
+    copy("v", C("BIT2"), C("PA", 5, 7))
+    gather("s", C("LB", 192, CW), C("land1", 0, 20), C("OU", 12, 22))
+    copy("s", R3("VROW"), bank(0, P, 0, 96))
+    gather("v", C("LB", 0, 192), C("land1", 0, 20), C("OU", 0, 12))
+    tr(C("LT", 0, 192), C("LB", 0, 192))
+    tr(C("LT", 192, CW), C("LB", 192, CW))
+    signs()
+    against(vb)
+    gather("s", C("VAL"), C("VROW"), C("OFV"))
+    against(vb + 1)
+    tally(vb)
+    against(vb + 2)
+    tally(vb + 1)
+    against(vb + 3)
+    tally(vb + 2)
+    tally(vb + 3)
+    tt(H("PB", vb, vb + 4), H("SCN", HW - 1, None, HW), U("SCN", HW - 1, None, HW), ALU.add)
+    tt(H("PB", sb_, sb_ + 2), H("LS"), U("LS"), ALU.add)
+    for q in range(2):
+        tt(Q("PZ", q), Q("PB", 0), Q("PB", 1), ALU.add)
+    ts(H("OFZ"), H("PZ"), float(4 * LOW + K), ALU.add)
+    ts(U("OFZ"), H("PZ"), H("QS2"), ALU.add)
+    scatter(C("RS"), C("OFZ"), C("VAL"))
+    tr(C("ET"), C("RS", 64, 192))
+    o = 4 * r
+    tt(C("land2", o, o + 2), C("ET", 0, 64, step=32), C("ET", 16, 64, step=32), ALU.add)
+    for q in range(3):
+        a = 64 * (q // 2)
+        tt(Q("land2", q, o + 2, o + 4), Q("ET", 3, a, a + 64, 32), Q("ET", 3, a + 16, a + 64, 32), ALU.add)
+    fan(C("land2", o, o + 4), "land2", 4, "ar2")
+    arrive("ar2", arrivals(), [C("land2", 0, o), C("land2", o + 4, 32)])
 
-    def slots(v):
-        for k in range(6):
-            val = C("V2C", k, k + 1) if v == 1 else C("VALT", 32 * k, 32 * k + 1)
-            ts(C("EV", 192 * v + 32 * k, 192 * v + 32 * k + 32), C("SLT2" if v == 1 else "SLT"), C("PZ", k, k + 1), ALU.is_equal, val, ALU.mult)
-    slots(1)
-    tr(U("VALT"), bank(4, P, 64, 128))
-    tr(C("ET", 192, 384), C("EV", 192, 384))
-    slots(2)
-    tr(C("ET", 0, 192), C("EV", 0, 192))
-    tr(C("ET", 384, 576), C("EV", 384, 576))
-    total_of("s", H("land2", 380, 381), H("ET", 192, 384), H("J3", 192, 384))
-    total_of("s", U("land2", 382, 383), U("ET", 192, 384), U("J3", 192, 384))
-    copy("s", U("land2", 380, 381), H("land2", 380, 381))
-    copy("s", H("land2", 382, 383), U("land2", 382, 383))
-    for v, at in ((0, 3), (2, 1)):
-        pairsum((T.land2[:, at:384:4], "land2", 0, 128, 380 + at, 381 + at), C("ET", 192 * v, 192 * v + 96), C("ET", 192 * v + 96, 192 * v + 192))
-    fan(C("land2", 380, 384), "land2", 384, 4, "ar2")
-    arrive("ar2", arrivals(), [C("land2", 384, 412)])
-
-    iota(C("RA", e0 - 8, e0 + 232), [[0, 240]], 0, 0)
-    iota(C("RB", e0 - 8, e0 + 232), [[0, 240]], 0, 0)
-    iota(C("INI"), [[0, 1]], 0, 0)
-    iota(C("RA", e0 - 8, e0 + 232, 0, 16), [[0, 240]], -2, 0)
-    iota(C("INI", 0, 1, 0, 16), [[0, 1]], 320 - 2 * (E * r - ws - 1), 0)
-    for t, x in (("VA", 1), ("VB", 0)):
-        iota(H(t, 0, 32), [[0, 32]], -2 * Wn, 0)
-        iota(U(t, 0, 32), [[2 * G3 - 4 * Wn, 2], [0, 16]], -2 * G3 + 2 * x, 0)
-    iota(C("VA", 0, 32, 0, 16), [[0, 32]], -2 * Wn - 2, 0)
-    iota(H("SEC"), [[0, 32]], 0, 0)
-    iota(U("SEC"), [[0, 32]], 1, 0)
-    iota(C("ZT"), [[0, 32]], 0, 0)
+    need("y", "ar1", total["ar1"], {})
+    dma("y", C("WB"), ext(T.w[:, :]))
+    fill(Q("FB", 3), 0)
+    fill(R3("RA", e0, e0 + 224), 0)
+    fill(Q("RA", 3, e0, e0 + 224), -1)
+    fill(R3("INI"), 0)
+    fill(Q("INI", 3), 193 - (E * r - ws - 1))
+    fill(Q("XS", 3, 240, 272), 0)
+    fill(C("ONE"), 1)
+    fill(C("XS", 0, 16), 0)
+    fill(C("M4"), 1)
+    iota(C("M4", 0, 60, step=4), [[0, 15]], 0, 0)
+    fill(C("ZT", 23, 32), 0)
     for k in range(3):
         iota(C("HT", k * Wn, k * Wn + Wn), [[4, Wn]], 4 * ws + 2 * (k // 2), 0)
     iota(C("HT", G3, G3 + Wn), [[4, Wn]], 4 * ws + 1, 0)
     ks, kn = (0, hL + hR) if hq == "HQ" else (0 if hL else Wn - 128, 128)
-    kids(hq, ks, kn, "FH1", "FH2", 5, "ssvsvssv")
-    affine(C("CT", 0, 16), C("CTI", 0, 16), C("CLM"), 1.0)
-    affine(C("CT", 16, 32), C("CTI", 16, 32), C("CLB"), 1.0)
+    kids(hq, ks, kn, "FH1", "FH2", (5, 6, 7, 0, 1, 2), "ssvsvssv")
+    affine(C("CA"), M0, -0.5, 1.0)
+    affine(C("CK"), M1, 272.0, -1.0)
+    affine(C("GB"), M0, float(-ws), -0.5)
+    affine(C("MB"), M1, BIG, -BIG)
+    affine(C("Y0"), M0, 0.0, float(-2 * Wn))
+    affine(C("DT"), C("ISC"), 256.0, float(2 * G3 - 2 * Wn - 256))
+    affine(C("CB0"), B16, 0.0, 2.0)
+    affine(C("YB"), M1, C("Y0"), float(-4 * Wn))
+    affine(C("CB"), M1, C("CB0"), 129.0)
+    affine(C("BM"), B8, 0.0, 0.125)
+    affine(C("AM"), B8, 1.0, -0.125)
+    affine(C("AM2"), B8, 2.0, -0.25)
+    affine(C("DL"), C("YB"), C("DT"), -1.0)
+    affine(C("YD"), C("AM2"), 0.0, M1)
+    affine(C("MSK"), C("TI", 0, 224), C("AM"), 0.0)
+    affine(C("YC"), C("YB"), C("YD"), C("BM"))
+    affine(C("LF", 0, 1), C("BIT2", 0, 1), C("BIT2", 1, 2), 9.0)
+    affine(C("LF", 1, 2), C("BIT2", 0, 1), 0.5, -17.0 / 16)
+    affine(H("CT"), H("CTI"), H("CB"), 1.0)
+    affine(U("CT"), U("CTI"), float(2 * G3), 0.0)
     quant("HK1", 0, kn, C("FH1", 0, 4 * kn))
     quant("HK2", 0, kn, C("FH2", 0, 4 * kn))
     if hq == "HQ":
@@ -506,95 +529,93 @@ def rank_program(g, core, T, topo):
         move("W1", k * Wn + hL + P, "HK%d" % k, kn - hR, hR)
     move("W2", 0, "W1", 0, 3 * Wn)
     move("W2", G3, "W1", 2 * Wn, Wn)
-    ts(C("OD"), C("OI2", 0, 20), PM16, ALU.add)
-    ts(C("OV"), C("OI2", 20, 22), IC, ALU.add)
+    ts(C("OD"), C("OI2"), PM16, ALU.add)
+    ts(Q("OFF", 3), Q("OI2", 3, 0, 8, 2), Q("BITS", 3, 1, 2), ALU.add, float(DUMP), ALU.add)
+    ts(H("OVK"), H("PINF", 0, 2), H("BITS", 0, 1), ALU.subtract)
+    memset(U("OVK"), 192)
+    ts(C("OLF", 0, 1), C("LF", 1, 2), B16, ALU.mult, C("LF", 0, 1), ALU.add)
     quant("WQ", 0, 128, C("WB"))
 
-    for k in range(2):
-        total_of("s", C("VV", k + 2, k + 3), C("land2", 382 + k, 412, step=4), C("JJ", 8 * k, 8 * k + 8))
-        total_of("v", C("VV", k, k + 1), C("land2", 380 + k, 412, step=4))
-    for k in range(2):
-        ts(C("RBS", 32 * k, 32 * k + 32), C("C64"), 0.0, ALU.mult, C("VV", k, k + 1), ALU.add)
-        affine(C("RBK", 32 * k, 32 * k + 32), C("C64"), C("VV", k + 2, k + 3), 0.0)
-    affine(C("TK"), C("VV", 2, 3), 0.0, TAU)
-    affine(C("KB"), C("VV", 3, 4), -BIG, 1.0)
-    affine(C("NB"), C("VV", 2, 3), -BIG, 1.0)
-    tr(C("SC", 0, 64), C("RBS"))
-    tr(C("KY", 0, 64), C("RBK"))
-    swap("SC")
-    swap("KY")
-    pairs("SC", "vsvs")
-    pairs("KY", "vsvs")
-    affine(C("E1"), C("SC"), C("VV", 1, 2), -1.0)
-    ts(C("NK1"), C("KY"), C("VV", 3, 4), ALU.subtract, -TAU, ALU.mult)
-    affine(C("E2"), C("SC", 32, 192), C("VV", 0, 1), -1.0)
-    affine(C("NK2"), C("KY", 32, 192), C("TK"), -TAU)
-    tt(C("M1"), C("E1"), C("NK1"), ALU.is_lt)
-    tt(C("M2"), C("E2"), C("NK2"), ALU.is_lt)
-    pairsum(C("R1"), C("M1", 0, 96), C("M1", 96, 192))
-    pairsum(C("R2"), C("M2", 0, 80), C("M2", 80, 160))
-    R1, R2 = C("R1", 95, 96), C("R2", 79, 80)
-    gathered(C("GD"), C("KY"), C("OD", 4, 12), float(-ws), 0.5, ACT.Relu)
-    for f, a in ((H, 64), (U, 32)):
-        affine(f("FR", 192, 224), f("KY", a, a + 32), -BIG, 1.0)
-        affine(f("FR", 224, 256), f("KY", a + 96, a + 128), -BIG, 1.0)
+    for b in (1, 0):
+        pairsum(C("RBS", 32 * b, 32 * b + 39), C("land2", b, b + 153, step=4), C("ZF", 0, 39))
+        pairsum(C("RBK", 32 * b, 32 * b + 39), C("land2", 2 + b, 2 + b + 153, step=4), C("ZF", 0, 39), M1)
+    sc = [R3("RBS", 32 * b + 38, 32 * b + 39) for b in range(2)]
+    ky = [R3("RBK", 32 * b + 38, 32 * b + 39) for b in range(2)]
+    both = R3("RBK", 38, 71, 32)
+    tr(C("SC", 0, 64), C("RBS", 7, 71))
+    tr(C("KY", 0, 64), C("RBK", 7, 71))
+    affine(R3("TK"), ky[1], 0.0, EPS)
+    affine(R3("KB"), both, -BIG, 1.0)
+    spread("SC", "svsvsv")
+    spread("KY", "vsvsvs")
+    affine(R3("E1", 0, P), R3("SC"), sc[0], -1.0, ACT.Sign)
+    ts(R3("KD", 0, P), R3("KY", 0, P), ky[0], ALU.subtract, -EPS, ALU.mult)
+    affine(R3("E1", P, 2 * P), R3("SC"), sc[1], -1.0, ACT.Sign)
+    affine(R3("KD", P, 2 * P), R3("KY", 0, P), R3("TK"), -EPS)
+    copy("v", Q("KY", 3, 64, 128), Q("KY", 0, 0, 64))
+    tt(R3("M1", 0, P), R3("E1", 0, P), R3("KD", 0, P), ALU.is_lt)
+    tt_by(C("V2"), C("KY"), C("OVK"), C("CT"), ALU.subtract)
+    pairsum(R3("RR", 0, 96), R3("M1", 0, 96), R3("M1", 96, P))
+    tt(R3("M1", P, 2 * P), R3("E1", P, 2 * P), R3("KD", P, 2 * P), ALU.is_lt)
+    ts(R3("FB", 0, 32), R3("C64"), R3("RR", 95, 96), ALU.is_gt, R3("KB", 0, 1), ALU.mult)
+    pairsum(R3("RR", 96, P), R3("M1", P, P + 96), R3("M1", P + 96, 2 * P))
+    gathered(C("GD"), C("KY", 64, 128), C("OD"), C("GB"), 0.5, ACT.Relu)
     affine(C("GE"), C("GD"), float(Wn - 1), -1.0, ACT.Relu)
-    affine(C("NKA"), C("VV", 2, 3), C("CN"), 1.0)
-    affine(C("Q1", 192, 256), C("FR", 192, 256), C("KB"), -1.0, ACT.Sign, C("S1A"))
-    affine(C("Q2", 192, 256), C("FR", 192, 256), C("NB"), -1.0, ACT.Sign, C("C2A"))
-    affine(C("KES"), C("VV", 3, 4), C("S1A"), 1.0)
-    affine(C("NKE"), C("NKA"), C("C2A"), 1.0)
-    for k in range(3):
-        affine(C("KE", k, k + 1), C("KES"), float(272 + 2 * k * DUMP), 1.0)
-    ts(C("FB", 32, 64), C("C64"), R1, ALU.is_gt, C("KB"), ALU.mult)
-    ts(C("FB", 0, 32), C("THT"), R2, ALU.is_gt, C("NB"), ALU.mult)
-    ts(C("FL"), C("C64", 0, 1), R1, ALU.is_gt)
-    ts(C("F2"), C("THT", 0, 1), R2, ALU.is_gt)
-    tr(C("FR", 0, 64), C("FB"))
+    affine(R3("TA"), both, R3("CA"), 1.0)
+    affine(R3("KC"), both, R3("CK"), 1.0)
+    affine(R3("KBH"), both, -BIG - 0.5, 1.0)
+    for b in range(2):
+        affine(R3("JA", 64 * b, 64 * b + 64), R3("KY", 64, 128), R3("TA", b, b + 1), -1.0, ACT.Sign, R3("SA", b, b + 1))
+    affine(C("XY"), C("V2"), C("DL"), 1.0)
+    affine(C("VA", 32, 64), C("V2"), C("AM2"), C("BM"))
+    for b in range(2):
+        affine(R3("KK", b, b + 1), R3("KC", b, b + 1), R3("SA", b, b + 1), 1.0)
+    affine(R3("KEP"), R3("KK", 0, 2), 2.0, 1.0)
     tr(C("GT"), C("GE"))
-    swap("FR")
+    ts(R3("FB", 32, 64), R3("C64"), R3("RR", 191, 192), ALU.is_gt, R3("KB", 1, 2), ALU.mult)
+    ts(R3("GG"), R3("RR", 95, P, 96), 64.0, ALU.is_ge, 2.0 * DUMP, ALU.mult)
+    tr(C("FR", 0, 64), C("FB"))
+    spread("FR", "svsvsv")
+    for b in range(2):
+        affine(R3("JB", P * b, P * b + P), R3("FR"), R3("KBH", b, b + 1), -1.0, ACT.Sign, R3("SB", b, b + 1))
     for k in (0, 1):
         ts(C("OFFG", 4 * k, 4 * k + 4), C("GT", 0, 128, step=32), -1.0, ALU.mult, float((2 + k) * Wn - 1), ALU.add)
-    pairs("FR", "vsvs")
-    affine(C("Q1", 0, 192), C("FR", 0, 192), C("KB"), -1.0, ACT.Sign, C("S1"))
-    affine(C("Q2", 0, 192), C("FR", 0, 192), C("NB"), -1.0, ACT.Sign, C("C2"))
-    win, off, ct = C("KY", 0, 96), C("OV"), C("CT")
-    run("v", lambda: g.vector.tensor_tensor(T.VA[:, 32:64], win[0].indirect(off[0]), ct[0], ALU.subtract), [win, off, ct], [C("VA", 32, 64)])
-    for k, x in enumerate((2 * DUMP - 1, -2 * DUMP - 1, 1 - 4 * DUMP)):
-        ts(C("DB", k, k + 1), C("FL"), float(x), ALU.mult, C("KE", k, k + 1), ALU.add)
-    ts(C("DBN"), C("F2"), -6.0 * DUMP - 1, ALU.mult, C("NKE"), ALU.add)
-    tt(C("VB", 32, 64), C("VA", 32, 64), C("BLT"), ALU.add)
+    tt_by(C("WW"), C("FR", 0, 64), C("OFV", 0, 2), C("XY"), ALU.max)
+    tt(R3("KK", 2, 4), R3("GG"), R3("KEP"), ALU.add)
+    ts(C("VA", 0, 32), C("WW"), C("BM"), ALU.mult, C("YC"), ALU.add)
     pick_codes("PK", 0, 128, "W1", 3 * Wn, C("OFFG"))
-    ts(C("OFF", 1, 4), C("DB"), C("S1"), ALU.add, 0.5, ALU.mult)
-    ts(C("OFF", 0, 1), C("C2"), C("DBN"), ALU.add, 0.5, ALU.mult)
+    for b in range(2):
+        o = (T.OFF[0:96, b:4:2], "OFF", 0, 96, 2 * b, 2 * b + 2)
+        ts(o, R3("KK", b, 4, 2), R3("SB", b, b + 1), ALU.add, 0.5, ALU.mult)
 
-    scatter(C("RB"), C("OFF"), C("VB"))
     scatter(C("RA"), C("OFF"), C("VA"))
-    affine(C("EB"), C("S1"), float(2 * e0 - 1), -1.0)
-    affine(C("BN"), C("DBN"), float(2 * e0 - 1), -1.0)
-    affine(C("JK", 0, 2), C("DB", 0, 2), C("EB"), -1.0, ACT.Sign, C("A12"))
-    affine(C("SGN"), C("C2"), C("BN"), -1.0, ACT.Sign)
-    affine(C("SB1"), C("DB", 2, 3), C("EB"), -1.0, ACT.Sign)
-    affine(C("AN"), C("SGN"), C("A12"), 1.0)
+    affine(R3("KK", 4, 6), R3("KK", 0, 2), R3("MB"), 1.0)
+    affine(R3("EB"), R3("SB"), float(2 * e0 - 1), -1.0)
     pick_scales("PK", 0, 128, "W1", 3 * Wn, C("OFFG"))
-    scaled("s", C("RB", e0 - 1, e0), C("RB", e0 - 1, e0), 0.0)
-    affine(C("XS", 224, 256), C("SEC"), C("SB1"), C("AN"))
-    xa, xb, x0, xo = C("RA", e0, e0 + 224), C("RB", e0 - 1, e0 + 223), C("INI"), C("XS", 0, 224)
-    run("v", lambda: g.vector.tensor_tensor_scan(xo[0], xa[0], xb[0], x0[0], ALU.add, ALU.subtract), [xa, xb, x0], [xo])
-    tr(C("XT"), C("XS"))
-    gathered(C("HT", G1, G1 + 128), C("KY"), C("OD", 12, 20), 0.0, 2.0, ACT.Identity)
-    total_of("s", C("ZS", 7, 8), C("XT", 224, 256), C("J3", 0, 32))
-    tt(C("ZS", 0, 7), C("XT", 0, 224, step=32), C("XT", 16, 224, step=32), ALU.add)
-    kids("PK", 0, 128, "GH1", "GH2", 5, "ssssssss")
-    quadsum("ZT", "HS", H("ZS"), U("ZS"), 8)
-    tr(C("XR"), C("ZT"))
+    for b in range(2):
+        affine(R3("JK", 2 * b, 2 * b + 2), R3("KK", 2 + b, 6, 2), R3("EB", b, b + 1), -1.0, ACT.Sign, R3("AA", b, b + 1))
+    affine(R3("XS", 240, 272), R3("ONE"), R3("AA", 1, 2), R3("AA", 0, 1))
+
+    def runs(o, keep, x, start):
+        s = start[0] if isinstance(start, tuple) else start
+        run("v", lambda: g.vector.tensor_tensor_scan(o[0], keep[0], x[0], s, ALU.mult, ALU.add),
+            [keep, x] + ([start] if isinstance(start, tuple) else []), [o])
+    runs(C("XS", 16, 240), C("MSK"), C("RA", e0, e0 + 224), C("INI"))
+    tr(C("XT", 0, 256), C("XS", 16, 272))
+    tr(C("XT", 256, 480), C("XS", 0, 224))
+    kids("PK", 0, 128, "GH1", "GH2", (5, 6, 7, 0, 1, 2, 3, 4), "ssssssss", range(4))
+    total_of(C("ZS", 3, 4), C("XT", 224, 256), C("J3"))
+    runs(C("ZS", 4, 64), C("M4"), C("XT", 0, 480, step=8), 0.0)
+    kids("PK", 0, 128, "GH1", "GH2", (5, 6, 7, 0, 1, 2, 3, 4), "ssssssss", range(4, 8))
     quant("W2", G1, G1 + 128, C("GH1"))
-    gather("v", C("YY"), C("XR"), C("OD", 0, 4))
-    tr(C("YT"), C("YY"))
+    tt(H("HS"), H("ZS", 3, 64, 4), U("ZS", 3, 64, 4), ALU.add)
+    for q in range(4):
+        tt(Q("ZT", q, 7, 23), Q("HS", 0), Q("HS", 1), ALU.add)
+    win, off, last = C("ZT", 8, 32), C("OLF", 0, 1), C("ZT", 7, 8)
+    run("v", lambda: g.vector.tensor_scalar(T.OFFL[:, :], win[0].indirect(off[0]), last[0], -0.5, ALU.add, ALU.mult), [win, off, last], [C("OFFL")])
     quant("W2", G2, G2 + 128, C("GH2"))
-    for h in (0, 1):
-        ts(part_of("OFFL", h, 14, 2), C("YT", 32 * h, 32 * h + 7), C("ZT", 7, 8), ALU.add, -0.5, ALU.mult)
-    affine(C("HT", G2, G2 + 128), C("HT", G1, G1 + 128), 1.0, 1.0)
+    affine(C("HT", G1, G1 + 128), C("KY", 0, 128), 0.0, 2.0)
+    affine(C("HT", G2, G2 + 128), C("KY", 0, 128), 1.0, 2.0)
     for c0, c1 in ((0, 128), (128, E)):
         off = C("OFFL", c0 // 16, c1 // 16)
         pick_codes("FQ", c0, c1, "W2", G3 + Wn, off)
@@ -612,6 +633,6 @@ def rank_program(g, core, T, topo):
     dma("s", ext(T.hs[:, :]), C("HR", 0, E, 0, 1))
 
     total["loc"] = loc[0]
-    for sem in SEMAPHORES:
-        if total.get(sem):
+    for sem in SEMAPHORES[4:] + SEMAPHORES[:4]:
+        if total.get(sem) and all(known[q].get(sem, 0) < total[sem] for q in known):
             need("g", sem, total[sem], {})

from concourse.bass import DstId, RemoteDMATransfer
from concourse.mybir import dt, AluOpType, AxisListType, ActivationFunctionType

ALU = AluOpType
ACT = ActivationFunctionType
N, P, K, E = 8, 192, 64, 208
WMAX = 336
TAU = 2.0 ** -106
EPS = 2.0 ** -13
BIG = 65536.0
DUMP = 1720
ROW = 8 + 2 * DUMP
CW = 352
HW = CW // 2
LOW = 256

SMALL = {}
for _n, _w in dict(PB=6, PZ=6, LO=2, HI=2, NST=2, LS=2, LM=2, LAM=6, PINF=6, BITS=5, MQ=4, ISC=1, U4F=4, QS2=1, KB0=1, CA=1, CK=1,
                   GB=1, MB=1, Y0=1, YB=1, YC=1, YD=1, AM=1, AM2=1, BM=1, DT=1, DL=1, CB0=1, CB=1, TK=1, KB=2, KBH=2, TA=2, SA=2,
                   KC=2, KK=6, KEP=2, GG=2, SB=2, EB=2, AA=2, INI=1, ZS=64, HS=16, JK=8, BIT2=2, LF=2).items():
    SMALL[_n] = (8 * sum((w + 7) // 8 for _, w in SMALL.values()), _w)


def _scratch():
    f, h, q, s = "float32", "bfloat16", "float8_e4m3fn_x4", "uint8"
    d = {}

    def sb(dtype, **kw):
        for name, n in kw.items():
            d[name] = ("sbuf", [128, n], dtype)
    sb(h, XB=4 * P, U4=4, UB=2048, AB=2048, BB=2048, WB=512, KH1=4 * P, KH2=4 * P, FH1=576, FH2=576, GH1=512, GH2=512,
       CM=6 * CW, SCN=4 * HW, J1=2 * CW, MA=384, Z0=128, PMR=192, E1=384, KD=384, M1=384, JA=128, JB=384)
    for name, n in dict(HX=128, UQ=512, AQ=512, BQ=512, WQ=128, W1=3 * WMAX, HQ=144, HK1=144, HK2=144, PK=128, W2=4 * WMAX + 256, FQ=E).items():
        d[name] = ("sbuf", [128, n], q)
        d[name + "S"] = ("sbuf", [128, n], s)
    sb(f, C64=32, ONE=32, ZF=40, OC=8, ST0=192, TI=256, TIE=256, LA=192, land1=24, LB=352, LT=352, VROW=192, VAL=96, RS=1600, ET=128,
       land2=160, RBS=72, RBK=72, SC=192, KY=200, FB=64, FR=192, VA=64, V2=32, XY=32, WW=32, CTI=32, CT=32, RA=ROW, MSK=224, M4=60, RR=192,
       XS=272, XT=480, ZT=32, HT=4 * WMAX + 256, HR=E, GD=128, GE=128, GT=128, YS=E, J3=32, OI2=8,
       SM=8 * sum((w + 7) // 8 for _, w in SMALL.values()))
    sb("int32", OI=24, PIN=6, PA=7)
    sb("uint16", OU=22, OFV=6, OFZ=6, OVK=2, OD=8, OFF=4, OFFG=8, OFFL=16, OLF=2)
    d["PS"] = ("psum", [128, 4096], f)
    return d


SCRATCH = _scratch()
SEMAPHORES = ["cv", "cs", "ct", "cg", "loc", "ar1", "ar2", "arh"] + ["d%d" % i for i in range(40)]


def _halo(r):
    return (0 if r == 0 else 128 - 16 * r), (0 if r == N - 1 else 16 + 16 * r)


def _land(r):
    hL, hR = _halo(r)
    return ("HQ", 0, hL) if hL and hR else ("W1", 0, hL + P)


def rank_program(g, core, T, topo):
    r = T.rank_of(core)
    if r is None:
        return
    hL, hR = _halo(r)
    Wn = hL + P + hR
    ws = P * r - hL
    G1, G2, G3 = 3 * Wn, 3 * Wn + 128, 3 * Wn + 256
    e0 = E * r + 8
    q_of = {"v": g.vector, "s": g.scalar, "t": g.tensor, "g": g, "y": g.sync}
    cnt = {"cv": 0, "cs": 0, "ct": 0, "cg": 0}
    known = {k: {} for k in q_of}
    recs = {}
    total = {}
    ndma, loc = [0], [0]

    def C(name, c0=0, c1=None, p0=0, p1=128, step=1):
        if name in SMALL:
            o, w = SMALL[name]
            c0, c1, name = o + c0, o + (w if c1 is None else c1), "SM"
        elif c1 is None:
            c1 = SCRATCH[name][1][-1]
        ap = T[name][p0:p1, c0:c1] if step == 1 else T[name][p0:p1, c0:c1:step]
        return (ap, name, p0, p1, c0, c1)

    def H(name, c0=0, c1=None, step=1):
        return C(name, c0, c1, 0, 64, step)

    def U(name, c0=0, c1=None, step=1):
        return C(name, c0, c1, 64, 128, step)

    def Q(name, q, c0=0, c1=None, step=1):
        return C(name, c0, c1, 32 * q, 32 * q + 32, step)

    def R3(name, c0=0, c1=None, step=1):
        return C(name, c0, c1, 0, 96, step)

    def part_of(name, i, n, step, c0=0):
        w = n // step
        return (T[name][:, c0 + i:c0 + n:step], name, 0, 128, c0 + i * w, c0 + i * w + w)

    def bank(k, n, p0=0, p1=128, c0=0):
        return (T.PS[p0:p1, 512 * k + c0:512 * k + n], "PS", 0, 128, 512 * k, 512 * k + 512)

    def ext(ap):
        return (ap, None, 0, 0, 0, 0)

    def need(q, sem, val, snap):
        if known[q].get(sem, 0) >= val:
            return
        q_of[q].wait_ge(T.sem[sem], val)
        for k, x in list(snap.items()) + [(sem, val)]:
            known[q][k] = max(known[q].get(k, 0), x)

    def deps(q, reads, writes):
        todo = {}
        for view, wr in [(x, False) for x in reads] + [(x, True) for x in writes]:
            _, name, p0, p1, c0, c1 = view
            for (a0, a1, b0, b1, kind, rq, sem, val, snap) in recs.get(name, []):
                if a0 >= p1 or p0 >= a1 or b0 >= c1 or c0 >= b1:
                    continue
                if not kind and (rq == q or (not wr and name != "PS")):
                    continue
                if val > todo.get(sem, (0, 0))[0]:
                    todo[sem] = (val, snap)
        for sem in sorted(todo, key=lambda k: -len(todo[k][1])):
            need(q, sem, todo[sem][0], todo[sem][1])

    def note(q, rq, sem, val, reads, writes):
        snap = dict(known[q])
        snap[sem] = val
        for view, wr in [(x, False) for x in reads] + [(x, True) for x in writes]:
            _, name, p0, p1, c0, c1 = view
            lst = recs.setdefault(name, [])
            if wr:
                lst[:] = [x for x in lst if not (x[0] >= p0 and x[1] <= p1 and x[2] >= c0 and x[3] <= c1)]
            lst.append((p0, p1, c0, c1, wr, rq, sem, val, snap))
        total[sem] = val

    def run(q, f, reads, writes):
        deps(q, reads, writes)
        sem = "c" + q
        cnt[sem] += 1
        f().then_inc(T.sem[sem], 1)
        note(q, q, sem, cnt[sem], reads, writes)

    def dma(q, out, in_, bits=0):
        w, x = [out] if out[1] else [], [in_] if in_[1] else []
        deps(q, x, w)
        sem = "d%d" % ndma[0]
        ndma[0] += 1
        o = out[0].bitcast(dt.uint8) if bits & 1 else out[0]
        i = in_[0].bitcast(dt.uint8) if bits & 2 else in_[0]
        q_of[q].dma_start(o, i).then_inc(T.sem[sem], 16)
        note(q, "dma", sem, 16, x, w)

    def move(dst, d0, src, s0, n):
        if n:
            dma("y", C(dst, d0, d0 + n), C(src, s0, s0 + n), bits=3)
            dma("y", C(dst + "S", d0, d0 + n), C(src + "S", s0, s0 + n))

    def memset(o, val):
        run("v", lambda: g.vector.memset(o[0], val), [], [o])

    def copy(q, o, i):
        run(q, (lambda: g.vector.tensor_copy(o[0], i[0])) if q == "v" else (lambda: g.scalar.activation(o[0], i[0], ACT.Copy)), [i], [o])

    def scaled(q, o, i, f):
        run(q, (lambda: g.vector.tensor_scalar(o[0], i[0], f, None, ALU.mult)) if q == "v" else
            (lambda: g.scalar.activation(o[0], i[0], ACT.Copy, scale=f)), [i], [o])

    def ts(o, i, s1, op0, s2=None, op1=None):
        rd = [i] + [x for x in (s1, s2) if isinstance(x, tuple)]
        a = s1[0] if isinstance(s1, tuple) else s1
        b = s2[0] if isinstance(s2, tuple) else s2
        run("v", (lambda: g.vector.tensor_scalar(o[0], i[0], a, None, op0)) if op1 is None else
            (lambda: g.vector.tensor_scalar(o[0], i[0], a, b, op0, op1)), rd, [o])

    def tt(o, a, b, op):
        run("v", lambda: g.vector.tensor_tensor(o[0], a[0], b[0], op), [a, b], [o])

    def tt_by(o, win, off, b, op):
        src = win[0].indirect(off[0])
        run("v", lambda: g.vector.tensor_tensor(o[0], src, b[0], op), [win, off, b], [o])

    def tr(o, i):
        run("v", lambda: g.vector.transpose(o[0], i[0]), [i], [o])

    def total_of(o, i, junk):
        run("s", lambda: g.scalar.activation(junk[0], i[0], ACT.Copy, accum_out=o[0]), [i], [o, junk])

    def pairsum(o, a, b, start=0.0):
        s = start[0] if isinstance(start, tuple) else start
        run("v", lambda: g.vector.tensor_tensor_scan(o[0], a[0], b[0], s, ALU.add, ALU.add),
            [a, b] + ([start] if isinstance(start, tuple) else []), [o])

    def affine(o, i, bias, scale, func=ACT.Identity, acc=None):
        rd = [i] + [x for x in (bias, scale) if isinstance(x, tuple)]
        b = bias[0] if isinstance(bias, tuple) else bias
        a = scale[0] if isinstance(scale, tuple) else scale
        if acc is None:
            run("s", lambda: g.scalar.activation(o[0], i[0], func, bias=b, scale=a), rd, [o])
        else:
            run("s", lambda: g.scalar.activation(o[0], i[0], func, bias=b, scale=a, accum_out=acc[0]), rd, [o, acc])

    def gather(q, o, win, off):
        src = win[0].indirect(off[0])
        run(q, (lambda: g.vector.tensor_copy(o[0], src)) if q == "v" else (lambda: g.scalar.activation(o[0], src, ACT.Copy)), [win, off], [o])

    def gathered(o, win, off, bias, scale, func):
        src = win[0].indirect(off[0])
        run("s", lambda: g.scalar.activation(o[0], src, func, bias=bias[0], scale=scale), [win, off, bias], [o])

    def scatter(win, off, i):
        run("v", lambda: g.vector.tensor_copy(win[0].indirect(off[0]), i[0]), [i, off], [win])

    def quant(name, c0, c1, src):
        o, s = C(name, c0, c1), C(name + "S", c0, c1)
        run("v", lambda: g.vector.quantize_mx(o[0], s[0], src[0]), [src], [o, s])

    def sides(l, lc, x, x0, x1):
        return [C(l, lc, lc + 128), C(l + "S", lc, lc + 128), C(x, x0, x1), C(x + "S", x0, x1)]

    def mm(o, *args):
        v = sides(*args)
        run("t", lambda: g.tensor.matmul_mx(o[0], v[0][0], v[1][0], v[2][0], v[3][0], True, True), v, [o])

    def mm2(o, first, second):
        v, w = sides(*first), sides(*second)

        def both():
            g.tensor.matmul_mx(o[0], v[0][0], v[1][0], v[2][0], v[3][0], True, False)
            return g.tensor.matmul_mx(o[0], w[0][0], w[1][0], w[2][0], w[3][0], False, True)
        run("t", both, v + w, [o])

    part = [False]

    def iota(o, pattern, base, cm, whole=False):
        now = o[3] - o[2] < 128
        if now or part[0]:
            need("g", "cg", cnt["cg"], {})
        part[0] = now
        run("g", (lambda: g.iota(o[0], pattern, base, cm)) if whole else
            (lambda: g.iota(o[0], pattern, base, cm, allow_small_or_imprecise_dtypes=True)), [], [o])

    def pick_codes(o, c0, c1, src, n, off):
        a, w = C(o, c0, c1), C(src, 0, n)
        run("v", lambda: g.vector.tensor_copy(a[0].bitcast(dt.uint32), w[0].bitcast(dt.uint32).indirect(off[0])), [w, off], [a])

    def pick_scales(o, c0, c1, src, n, off):
        gather("s", C(o + "S", c0, c1), C(src + "S", 0, n), off)

    def quadsum(o, h, lo, up, n):
        tt(H(h, 0, n), lo, up, ALU.add)
        for q in range(4):
            tt(Q(o, q, 0, n), Q(h, 0, 0, n), Q(h, 1, 0, n), ALU.add)

    def spread(name, order):
        for k, (to, at, of) in enumerate(((0, 1, 1), (1, 1, 0), (2, 1, 0), (0, 2, 2), (1, 2, 2), (2, 2, 1))):
            copy(order[k], Q(name, to, 64 * at, 64 * at + 64), Q(name, of, 0, 64))

    def kids(src, c0, n, t1, t2, banks, pat, steps=range(8)):
        for i in steps:
            k = banks[i % len(banks)]
            mm(bank(k, n), "AQ" if i < 4 else "BQ", 128 * (i % 4), src, c0, c0 + n)
            scaled(pat[i], part_of(t1 if i < 4 else t2, i % 4, 4 * n, 4), bank(k, n), 0.0625)

    def ways(a):
        return topo.engines(a, [c for c in T.cores if topo.chip(c) != topo.chip(a)][0])

    def split(a, b):
        if topo.chip(a) != topo.chip(b):
            return topo.engines(a, b)
        return [e for e in topo.engines(a, b) if e not in ways(a)][:2]

    def arrivals():
        return sum(len(split(c, core)) for c in T.cores if c != core)

    def fan(src, dst, width, arr):
        deps("g", [src], [])
        others = [c for c in T.cores if c != core]
        far = [c for c in others if topo.chip(c) != topo.chip(core)]
        near = [c for c in others if topo.chip(c) == topo.chip(core)]
        fe, ne = split(core, far[0]), split(core, near[0])

        def tf(dsts, eng):
            ids = []
            for c in dsts:
                rid, pid, _ = topo.addr(c)
                ids.append(DstId(rid=rid, pnc=pid))
            return RemoteDMATransfer(dst_ids=ids, dma_engine_mask=sum(1 << e for e in eng), remote_sem=T.sem[arr], srcs=[src[0]],
                                     dsts=[T[dst][:, width * r:width * r + width] for _ in dsts])
        g.remote_dma_fused([tf(far, fe), tf(near, ne)], local_sem=T.sem.loc)
        loc[0] += len(fe) + len(ne)

    def halo(d, sfx):
        c = T.cores[d]
        dst, a, b = _land(d)
        c0, c1, at = (P - _halo(d)[0], P, a) if d > r else (0, _halo(d)[1], b)
        rid, pid, _ = topo.addr(c)
        s = C("HX" + sfx, c0 - hx, c1 - hx) if d == early else C("W1" + sfx, hL + c0, hL + c1)
        deps("g", [s], [])
        o, i = T[dst + sfx][:, at:at + c1 - c0], s[0]
        if not sfx:
            o, i = o.bitcast(dt.uint8), i.bitcast(dt.uint8)
        g.remote_dma(o, i, T.sem.arh, T.sem.loc, pid, rid, sum(1 << e for e in ways(core)))
        loc[0] += len(ways(core))

    def arrive(sem, val, writes):
        for _, name, p0, p1, c0, c1 in writes:
            if c1 > c0:
                recs.setdefault(name, []).append((p0, p1, c0, c1, True, "far", sem, val, {sem: val}))
        total[sem] = val

    dma("s", C("U4"), ext(T.u[:, 0:4]))
    early = r - 1 if r else r + 1
    hx = 0 if r else P - 128
    for c0, c1 in ((hx, hx + 128), (128, P) if r else (0, hx)):
        dma("y", C("XB", 4 * c0, 4 * c1), ext(T.x[:, 4 * c0:4 * c1]))
    for name, t in (("AB", T.a), ("BB", T.b)):
        dma("y", C(name), ext(t[:, :]))

    iota(C("PIN"), [[32, 6]], 0, 1, True)
    iota(C("TI"), [[-1, 256]], 64, 1)
    iota(C("OI"), [[4, 4], [1, 3], [0, 2]], 0, 0, True)
    odd, pair = r % 2, r // 2
    skip = 6 * pair + 4 * odd
    cut = 32 * (3 * pair + 2 * odd)
    vb, sb_ = (2, 0) if odd else (0, 4)
    memset(C("Z0"), 0.0)
    memset(C("PMR", 0, 64), 1.0)
    memset(C("PMR", 64, 192), -1.0)
    copy("v", C("PINF"), C("PIN"))
    PID = C("PINF", 0, 1)
    for k, m in enumerate((96, 15, 32, 16, 8)):
        ts(C("PA", k, k + 1), C("PIN", 0, 1), m, ALU.bitwise_and)
    copy("v", C("BITS"), C("PA", 0, 5))
    QO, PM16, B32, B16, B8 = [C("BITS", k, k + 1) for k in range(5)]
    M0, M1 = C("MQ", 0, 1), C("MQ", 1, 2)
    for c in (1280, 1408, 1664, 1792, 1920):
        copy("s", C("UB", c, c + 128), C("Z0"))
    copy("s", C("U4F"), C("U4"))
    for t in range(4):
        affine(part_of("UB", t, 768, 4, 512), C("PMR"), 0.0, C("U4F", t, t + 1), ACT.Copy)
    scaled("s", C("TIE"), C("TI"), TAU)

    for t in range(4):
        ts(part_of("UB", t, 512, 4), C("Z0"), C("U4", t, t + 1), ALU.add)
    quant("HX", 0, 128, C("XB", 4 * hx, 4 * hx + 512))
    quant("UQ", 0, 128, C("UB", 0, 512))
    quant("W1", hL, hL + P, C("XB"))
    pieces = [(d, sfx) for sfx in ("S", "") for d in (r - 1, r + 1) if 0 <= d < N]
    halo(*pieces[0])
    mm(bank(1 if r else 2, 128), "HX", 0, "UQ", 0, 128)
    mm(bank(2 if r else 1, 128), "W1", hL + 64 - hx, "UQ", 0, 128)
    mm(bank(0, P), "UQ", 0, "W1", hL, hL + P)
    ts(C("ISC"), PID, 64.0, ALU.is_ge)
    quant("UQ", 128, 320, C("UB", 512, 1280))
    for k, c in ((3, 0), (4, 64)):
        mm2(bank(k, P), ("W1", hL + c, "UQ", 0, P), ("UQ", P, "W1", hL, hL + P))
    copy("s" if r else "v", C("OC", 0, 1), bank(1, 1))
    copy("v" if r else "s", C("OC", 1, 2), bank(2, 1))
    ts(C("MQ"), C("PINF", 0, 4), PID, ALU.subtract, QO, ALU.is_equal)
    ts(C("OFV"), C("PINF"), QO, ALU.subtract)
    for c0, c1, x in ((0, skip, 0), (skip, 22, 2)):
        if c1 > c0:
            ts(C("OU", c0, c1), C("OI", c0 + x, c1 + x), C("ISC"), ALU.add)
    memset(U("OU", skip - 2, skip) if odd else H("OU", skip, skip + 2), 16)
    fan(C("OC", 0, 2), "land1", 2, "ar1")
    arrive("ar1", arrivals(), [C("land1", 0, 16)])
    for piece in pieces[1:]:
        halo(*piece)
    want = sum(2 * len(ways(T.cores[d])) for d in (r - 1, r + 1) if 0 <= d < N)
    hq, hl, hr = _land(r)
    arrive("arh", want, [C(hq + x, a, b) for x in ("", "S") for a, b in ((hl, hl + hL), (hr, hr + hR))])

    def fill(o, val):
        iota(o, [[0, o[5] - o[4]]], val, 0)
    iota(C("OI2"), [[16, 4], [0, 2]], 0, 0)
    iota(C("CTI"), [[64, 2], [2, 16]], 2 * (G2 + ws), 0)
    fill(C("land2", 32, 160), 0)
    fill(C("ZF"), 0)
    fill(C("C64"), 64)
    fill(C("KY", 192, 200), 0)

    tr(C("ST0"), bank(0, P))
    memset(C("land1", 16, 20), -9e29)
    for t in range(4):
        affine(part_of("UB", t, 128, 4, 1536), C("PMR", 0, 32), 0.0, C("U4F", t, t + 1), ACT.Copy)
    affine(C("QS2"), B32, float(4 * LOW), 2.0)
    affine(C("KB0"), PID, float(2 * P * r), 2.0)
    for k in range(2):
        scaled("s", C("NST", k, k + 1), C("ST0", 32 * (sb_ + k), 32 * (sb_ + k) + 1), -1.0)
    affine(Q("VROW", 3), Q("TI", 3, 64, 256), Q("KB0", 3), -2.0)
    copy("s", C("RS", 64, 192), C("Z0"))
    copy("s", C("land2", 4 * r, 4 * r + 4), C("Z0", 0, 4))
    for c in (0, 256):
        quant("AQ", c, c + 256, C("AB", 4 * c, 4 * c + 1024))
    tt(C("MA", 0, P), bank(3, P), C("TIE", 64, 256), ALU.is_lt)
    tt(C("MA", P, 2 * P), bank(4, P), C("TIE", 0, P), ALU.is_lt)
    kids("W1", hL, P, "KH1", "KH2", (5, 6, 7, 1, 2), "ssssssss", range(4))
    for c in (0, 256):
        quant("BQ", c, c + 256, C("BB", 4 * c, 4 * c + 1024))
    for k in range(2):
        pairsum(C("LA", 96 * k, 96 * k + 96), C("MA", P * k, P * k + 96), C("MA", P * k + 96, P * k + P))
    quant("UQ", 320, 512, C("UB", 1280, 2048))
    kids("W1", hL, P, "KH1", "KH2", (5, 6, 7, 1, 2), "ssssssss", range(4, 8))

    def field(q, c, start, stop):
        v = sides("UQ", 384 - 32 * q, "W1", c, c + P)
        run("t", lambda: g.tensor.matmul_mx(bank(0, P)[0], v[0][0], v[1][0], v[2][0], v[3][0], start, stop), v, [bank(0, P)])
    for k in range(3):
        src, q0 = ((0, 0), (0, 2) if odd else (1, 0), (1, 2))[k]
        affine(C("LAM", 2 * k, 2 * k + 2), C("MQ", q0, q0 + 2), float((cut if 2 * k == sb_ else 0) - LOW), C("LA", 96 * src + 95, 96 * src + 96))

    def tally(k):
        i = k - vb
        pairsum(C("SCN", HW * i, HW * i + HW), C("CM", CW * k, CW * k + HW), C("CM", CW * k + HW, CW * k + CW), C("LAM", k, k + 1))

    def against(k):
        sc = C("ST0", 32 * k, 32 * k + 1)
        if cut > 0:
            ts(C("CM", CW * k, CW * k + cut), C("LT", 0, cut), sc, ALU.is_ge)
        if cut < CW:
            ts(C("CM", CW * k + cut, CW * k + CW), C("LT", cut, CW), sc, ALU.is_gt)

    def signs():
        lam = [C("LAM", sb_ + i, sb_ + i + 1) for i in range(2)]
        for i in range(2):
            affine(C("CM", CW * (sb_ + i), CW * (sb_ + i + 1)), C("LT"), C("NST", i, i + 1), 1.0, ACT.Sign)
        for i in range(2 if cut > 0 else 0):
            c, j = CW * (sb_ + i), CW * i
            affine(C("J1", j, j + cut), C("CM", c, c + cut), 0.0, -1.0, ACT.Relu, C("LO", i, i + 1))
        for i in range(2 if cut < CW else 0):
            c, j = CW * (sb_ + i), CW * i
            affine(C("J1", j + cut, j + CW), C("CM", c + cut, c + CW), 0.0, 1.0, ACT.Relu, C("HI", i, i + 1))
            if i == 0 and cut > 0:
                for k in range(2):
                    affine(C("LM", k, k + 1), C("LO", k, k + 1), lam[k], -1.0)
                lam = [C("LM", k, k + 1) for k in range(2)]
        for i in range(2):
            if cut < CW:
                affine(C("LS", i, i + 1), C("HI", i, i + 1), lam[i], 1.0)
            else:
                affine(C("LS", i, i + 1), C("LO", i, i + 1), lam[i], -1.0)

    field(2, hL, True, False)
    quant("W1", Wn + hL, Wn + hL + P, C("KH1"))
    field(0, Wn + hL, False, False)
    for k, (x, y) in enumerate(((1, 0), (15, 1))):
        ts(C("PA", 5 + k, 6 + k), C("PIN", 0, 1), x, ALU.bitwise_and, y, ALU.logical_shift_right)
    quant("W1", 2 * Wn + hL, 2 * Wn + hL + P, C("KH2"))
    field(1, 2 * Wn + hL, False, True)
    copy("v", C("BIT2"), C("PA", 5, 7))
    gather("s", C("LB", 192, CW), C("land1", 0, 20), C("OU", 12, 22))
    copy("s", R3("VROW"), bank(0, P, 0, 96))
    gather("v", C("LB", 0, 192), C("land1", 0, 20), C("OU", 0, 12))
    tr(C("LT", 0, 192), C("LB", 0, 192))
    tr(C("LT", 192, CW), C("LB", 192, CW))
    signs()
    against(vb)
    gather("s", C("VAL"), C("VROW"), C("OFV"))
    against(vb + 1)
    tally(vb)
    against(vb + 2)
    tally(vb + 1)
    against(vb + 3)
    tally(vb + 2)
    tally(vb + 3)
    tt(H("PB", vb, vb + 4), H("SCN", HW - 1, None, HW), U("SCN", HW - 1, None, HW), ALU.add)
    tt(H("PB", sb_, sb_ + 2), H("LS"), U("LS"), ALU.add)
    for q in range(2):
        tt(Q("PZ", q), Q("PB", 0), Q("PB", 1), ALU.add)
    ts(H("OFZ"), H("PZ"), float(4 * LOW + K), ALU.add)
    ts(U("OFZ"), H("PZ"), H("QS2"), ALU.add)
    scatter(C("RS"), C("OFZ"), C("VAL"))
    tr(C("ET"), C("RS", 64, 192))
    o = 4 * r
    tt(C("land2", o, o + 2), C("ET", 0, 64, step=32), C("ET", 16, 64, step=32), ALU.add)
    for q in range(3):
        a = 64 * (q // 2)
        tt(Q("land2", q, o + 2, o + 4), Q("ET", 3, a, a + 64, 32), Q("ET", 3, a + 16, a + 64, 32), ALU.add)
    fan(C("land2", o, o + 4), "land2", 4, "ar2")
    arrive("ar2", arrivals(), [C("land2", 0, o), C("land2", o + 4, 32)])

    need("y", "ar1", total["ar1"], {})
    dma("y", C("WB"), ext(T.w[:, :]))
    fill(Q("FB", 3), 0)
    fill(R3("RA", e0, e0 + 224), 0)
    fill(Q("RA", 3, e0, e0 + 224), -1)
    fill(R3("INI"), 0)
    fill(Q("INI", 3), 193 - (E * r - ws - 1))
    fill(Q("XS", 3, 240, 272), 0)
    fill(C("ONE"), 1)
    fill(C("XS", 0, 16), 0)
    fill(C("M4"), 1)
    iota(C("M4", 0, 60, step=4), [[0, 15]], 0, 0)
    fill(C("ZT", 23, 32), 0)
    for k in range(3):
        iota(C("HT", k * Wn, k * Wn + Wn), [[4, Wn]], 4 * ws + 2 * (k // 2), 0)
    iota(C("HT", G3, G3 + Wn), [[4, Wn]], 4 * ws + 1, 0)
    ks, kn = (0, hL + hR) if hq == "HQ" else (0 if hL else Wn - 128, 128)
    kids(hq, ks, kn, "FH1", "FH2", (5, 6, 7, 0, 1, 2), "ssvsvssv")
    affine(C("CA"), M0, -0.5, 1.0)
    affine(C("CK"), M1, 272.0, -1.0)
    affine(C("GB"), M0, float(-ws), -0.5)
    affine(C("MB"), M1, BIG, -BIG)
    affine(C("Y0"), M0, 0.0, float(-2 * Wn))
    affine(C("DT"), C("ISC"), 256.0, float(2 * G3 - 2 * Wn - 256))
    affine(C("CB0"), B16, 0.0, 2.0)
    affine(C("YB"), M1, C("Y0"), float(-4 * Wn))
    affine(C("CB"), M1, C("CB0"), 129.0)
    affine(C("BM"), B8, 0.0, 0.125)
    affine(C("AM"), B8, 1.0, -0.125)
    affine(C("AM2"), B8, 2.0, -0.25)
    affine(C("DL"), C("YB"), C("DT"), -1.0)
    affine(C("YD"), C("AM2"), 0.0, M1)
    affine(C("MSK"), C("TI", 0, 224), C("AM"), 0.0)
    affine(C("YC"), C("YB"), C("YD"), C("BM"))
    affine(C("LF", 0, 1), C("BIT2", 0, 1), C("BIT2", 1, 2), 9.0)
    affine(C("LF", 1, 2), C("BIT2", 0, 1), 0.5, -17.0 / 16)
    affine(H("CT"), H("CTI"), H("CB"), 1.0)
    affine(U("CT"), U("CTI"), float(2 * G3), 0.0)
    quant("HK1", 0, kn, C("FH1", 0, 4 * kn))
    quant("HK2", 0, kn, C("FH2", 0, 4 * kn))
    if hq == "HQ":
        move("W1", 0, "HQ", 0, hL)
        move("W1", hL + P, "HQ", hL, hR)
    for k in (1, 2):
        move("W1", k * Wn, "HK%d" % k, 0, hL)
        move("W1", k * Wn + hL + P, "HK%d" % k, kn - hR, hR)
    move("W2", 0, "W1", 0, 3 * Wn)
    move("W2", G3, "W1", 2 * Wn, Wn)
    ts(C("OD"), C("OI2"), PM16, ALU.add)
    ts(Q("OFF", 3), Q("OI2", 3, 0, 8, 2), Q("BITS", 3, 1, 2), ALU.add, float(DUMP), ALU.add)
    ts(H("OVK"), H("PINF", 0, 2), H("BITS", 0, 1), ALU.subtract)
    memset(U("OVK"), 192)
    ts(C("OLF", 0, 1), C("LF", 1, 2), B16, ALU.mult, C("LF", 0, 1), ALU.add)
    quant("WQ", 0, 128, C("WB"))

    for b in (1, 0):
        pairsum(C("RBS", 32 * b, 32 * b + 39), C("land2", b, b + 153, step=4), C("ZF", 0, 39))
        pairsum(C("RBK", 32 * b, 32 * b + 39), C("land2", 2 + b, 2 + b + 153, step=4), C("ZF", 0, 39), M1)
    sc = [R3("RBS", 32 * b + 38, 32 * b + 39) for b in range(2)]
    ky = [R3("RBK", 32 * b + 38, 32 * b + 39) for b in range(2)]
    both = R3("RBK", 38, 71, 32)
    tr(C("SC", 0, 64), C("RBS", 7, 71))
    tr(C("KY", 0, 64), C("RBK", 7, 71))
    affine(R3("TK"), ky[1], 0.0, EPS)
    affine(R3("KB"), both, -BIG, 1.0)
    spread("SC", "svsvsv")
    spread("KY", "vsvsvs")
    affine(R3("E1", 0, P), R3("SC"), sc[0], -1.0, ACT.Sign)
    ts(R3("KD", 0, P), R3("KY", 0, P), ky[0], ALU.subtract, -EPS, ALU.mult)
    affine(R3("E1", P, 2 * P), R3("SC"), sc[1], -1.0, ACT.Sign)
    affine(R3("KD", P, 2 * P), R3("KY", 0, P), R3("TK"), -EPS)
    copy("v", Q("KY", 3, 64, 128), Q("KY", 0, 0, 64))
    tt(R3("M1", 0, P), R3("E1", 0, P), R3("KD", 0, P), ALU.is_lt)
    tt_by(C("V2"), C("KY"), C("OVK"), C("CT"), ALU.subtract)
    pairsum(R3("RR", 0, 96), R3("M1", 0, 96), R3("M1", 96, P))
    tt(R3("M1", P, 2 * P), R3("E1", P, 2 * P), R3("KD", P, 2 * P), ALU.is_lt)
    ts(R3("FB", 0, 32), R3("C64"), R3("RR", 95, 96), ALU.is_gt, R3("KB", 0, 1), ALU.mult)
    pairsum(R3("RR", 96, P), R3("M1", P, P + 96), R3("M1", P + 96, 2 * P))
    gathered(C("GD"), C("KY", 64, 128), C("OD"), C("GB"), 0.5, ACT.Relu)
    affine(C("GE"), C("GD"), float(Wn - 1), -1.0, ACT.Relu)
    affine(R3("TA"), both, R3("CA"), 1.0)
    affine(R3("KC"), both, R3("CK"), 1.0)
    affine(R3("KBH"), both, -BIG - 0.5, 1.0)
    for b in range(2):
        affine(R3("JA", 64 * b, 64 * b + 64), R3("KY", 64, 128), R3("TA", b, b + 1), -1.0, ACT.Sign, R3("SA", b, b + 1))
    affine(C("XY"), C("V2"), C("DL"), 1.0)
    affine(C("VA", 32, 64), C("V2"), C("AM2"), C("BM"))
    for b in range(2):
        affine(R3("KK", b, b + 1), R3("KC", b, b + 1), R3("SA", b, b + 1), 1.0)
    affine(R3("KEP"), R3("KK", 0, 2), 2.0, 1.0)
    tr(C("GT"), C("GE"))
    ts(R3("FB", 32, 64), R3("C64"), R3("RR", 191, 192), ALU.is_gt, R3("KB", 1, 2), ALU.mult)
    ts(R3("GG"), R3("RR", 95, P, 96), 64.0, ALU.is_ge, 2.0 * DUMP, ALU.mult)
    tr(C("FR", 0, 64), C("FB"))
    spread("FR", "svsvsv")
    for b in range(2):
        affine(R3("JB", P * b, P * b + P), R3("FR"), R3("KBH", b, b + 1), -1.0, ACT.Sign, R3("SB", b, b + 1))
    for k in (0, 1):
        ts(C("OFFG", 4 * k, 4 * k + 4), C("GT", 0, 128, step=32), -1.0, ALU.mult, float((2 + k) * Wn - 1), ALU.add)
    tt_by(C("WW"), C("FR", 0, 64), C("OFV", 0, 2), C("XY"), ALU.max)
    tt(R3("KK", 2, 4), R3("GG"), R3("KEP"), ALU.add)
    ts(C("VA", 0, 32), C("WW"), C("BM"), ALU.mult, C("YC"), ALU.add)
    pick_codes("PK", 0, 128, "W1", 3 * Wn, C("OFFG"))
    for b in range(2):
        o = (T.OFF[0:96, b:4:2], "OFF", 0, 96, 2 * b, 2 * b + 2)
        ts(o, R3("KK", b, 4, 2), R3("SB", b, b + 1), ALU.add, 0.5, ALU.mult)

    scatter(C("RA"), C("OFF"), C("VA"))
    affine(R3("KK", 4, 6), R3("KK", 0, 2), R3("MB"), 1.0)
    affine(R3("EB"), R3("SB"), float(2 * e0 - 1), -1.0)
    pick_scales("PK", 0, 128, "W1", 3 * Wn, C("OFFG"))
    for b in range(2):
        affine(R3("JK", 2 * b, 2 * b + 2), R3("KK", 2 + b, 6, 2), R3("EB", b, b + 1), -1.0, ACT.Sign, R3("AA", b, b + 1))
    affine(R3("XS", 240, 272), R3("ONE"), R3("AA", 1, 2), R3("AA", 0, 1))

    def runs(o, keep, x, start):
        s = start[0] if isinstance(start, tuple) else start
        run("v", lambda: g.vector.tensor_tensor_scan(o[0], keep[0], x[0], s, ALU.mult, ALU.add),
            [keep, x] + ([start] if isinstance(start, tuple) else []), [o])
    runs(C("XS", 16, 240), C("MSK"), C("RA", e0, e0 + 224), C("INI"))
    tr(C("XT", 0, 256), C("XS", 16, 272))
    tr(C("XT", 256, 480), C("XS", 0, 224))
    kids("PK", 0, 128, "GH1", "GH2", (5, 6, 7, 0, 1, 2, 3, 4), "ssssssss", range(4))
    total_of(C("ZS", 3, 4), C("XT", 224, 256), C("J3"))
    runs(C("ZS", 4, 64), C("M4"), C("XT", 0, 480, step=8), 0.0)
    kids("PK", 0, 128, "GH1", "GH2", (5, 6, 7, 0, 1, 2, 3, 4), "ssssssss", range(4, 8))
    quant("W2", G1, G1 + 128, C("GH1"))
    tt(H("HS"), H("ZS", 3, 64, 4), U("ZS", 3, 64, 4), ALU.add)
    for q in range(4):
        tt(Q("ZT", q, 7, 23), Q("HS", 0), Q("HS", 1), ALU.add)
    win, off, last = C("ZT", 8, 32), C("OLF", 0, 1), C("ZT", 7, 8)
    run("v", lambda: g.vector.tensor_scalar(T.OFFL[:, :], win[0].indirect(off[0]), last[0], -0.5, ALU.add, ALU.mult), [win, off, last], [C("OFFL")])
    quant("W2", G2, G2 + 128, C("GH2"))
    affine(C("HT", G1, G1 + 128), C("KY", 0, 128), 0.0, 2.0)
    affine(C("HT", G2, G2 + 128), C("KY", 0, 128), 1.0, 2.0)
    for c0, c1 in ((0, 128), (128, E)):
        off = C("OFFL", c0 // 16, c1 // 16)
        pick_codes("FQ", c0, c1, "W2", G3 + Wn, off)
        pick_scales("FQ", c0, c1, "W2", G3 + Wn, off)
    mm(bank(0, 128), "WQ", 0, "FQ", 0, 128)
    mm(bank(1, 128), "WQ", 0, "FQ", E - 128, E)
    dma("y", ext(T.oc[:, :]), C("FQ"), bits=2)
    gather("s", C("HR"), C("HT", 0, G3 + Wn), C("OFFL", 0, 13))
    for k in range(4):
        dma("yyss"[k], ext(T.osc[4 * k:4 * k + 4, :]), C("FQS", 0, E, 32 * k, 32 * k + 4))
    copy("v", C("YS", 0, 128), bank(0, 128))
    dma("y", ext(T.y[:, 0:128]), C("YS", 0, 128))
    copy("v", C("YS", 128, E), bank(1, 128, 0, 128, 256 - E))
    dma("y", ext(T.y[:, 128:E]), C("YS", 128, E))
    dma("s", ext(T.hs[:, :]), C("HR", 0, E, 0, 1))

    total["loc"] = loc[0]
    for sem in SEMAPHORES[4:] + SEMAPHORES[:4]:
        if total.get(sem) and all(known[q].get(sem, 0) < total[sem] for q in known):
            need("g", sem, total[sem], {})
